import numpy as np, ml_dtypes
CORES = [16,18,20,22]
N = 4
import mx_ref
BF = ml_dtypes.bfloat16
def cols(t, e):
    v = np.concatenate([t.reshape(128, -1, 4), np.zeros((128, 1, 4), BF)], axis=1)
    return np.ascontiguousarray(v[:, e]).reshape(128, -1)
def f(rng, *shape):
    return mx_ref.flush((rng.standard_normal(shape, dtype=np.float32) * np.exp2(rng.integers(-2, 3, shape[:-1] + (1,)))).astype(BF))
def wide(rng, *shape, cols=0):
    v = rng.standard_normal(shape, dtype=np.float32) * np.exp2(rng.integers(-12, 13, shape)).astype(np.float32)
    if cols: v *= np.repeat(np.exp2(rng.integers(-cols, cols + 1, shape[:-2] + (1, shape[-1] // 4))) * (rng.random(shape[:-2] + (1, shape[-1] // 4)) > 0.0625), 4, axis=-1).astype(np.float32)
    return mx_ref.flush(v.astype(BF))
T, K, O = 512, 256, 4
def setup_inputs(rng):
    u = np.zeros((128, 512), BF); u[:, :4] = f(rng, 128, 4)
    return {"x": f(rng, N, 128, 4 * T), "u": np.stack([u] * N), "w": f(rng, N, 128, 512 * O)}
def signs(d):
    return np.where(d["u"][0][:, :4].astype(np.float32) < 0, -1, 1).astype(np.float32)
def blocks(rng, n):
    return np.repeat(rng.permutation(16) < n, 8)
def plant(rng, d, n):
    for s in range(N):
        v = d["x"][s].astype(np.float32).reshape(128, T, 4)
        k = rng.permutation(T)[:n[s]]
        v[:, k] = np.abs(v[:, k]) * signs(d)[:, None] * np.float32(8)
        d["x"][s] = v.reshape(128, -1).astype(BF)
    return d
def setup_inputs_one(rng):
    d = setup_inputs(rng); return plant(rng, d, np.where(np.arange(N) == rng.integers(0, N), K, 0))
def setup_inputs_zeros(rng):
    d = setup_inputs(rng); m = blocks(rng, 2)
    d["u"][:, ~m] = 0
    k = rng.permutation(N * T); g = np.full(N * T, -1, np.float32)
    g[k[:K // 3]] = 1; g[k[K // 3:2 * (K // 3)]] = 0
    v = np.abs(d["x"][:, m].astype(np.float32)).reshape(N, -1, T, 4)
    d["x"][:, m] = (v * signs(d)[m][:, None] * g.reshape(N, 1, T, 1)).reshape(N, -1, 4 * T).astype(BF)
    return d
def setup_inputs_few(rng):
    d = setup_inputs(rng); p = rng.permutation(N); g = p[N - N // 2:]
    d["x"][g] = (-np.abs(d["x"][g].astype(np.float32)) * np.tile(signs(d), (1, T))).astype(BF)
    n = np.zeros(N, int); n[p[:2]] = [K * 3 // 5, K - K * 3 // 5]
    return plant(rng, d, n)
def setup_inputs_ties(rng):
    d = setup_inputs(rng); b = f(rng, 128, 4 * 20); m = blocks(rng, 4)
    d["u"][:, m] = 0
    d["x"] = np.stack([cols(b, rng.permutation(np.arange(T) % 20)) for r in range(N)])
    d["x"][:, m] = f(rng, N, 32, 4 * T); return d
def setup_inputs_spread(rng):
    d = setup_inputs(rng); d["x"] = wide(rng, N, 128, 4 * T, cols=8); return d
def check_inputs(d):
    b = []
    u = d["u"].astype(np.float32)
    if (u != u[:1]).any(): b.append("u_same")
    if (u[:, :, 4:] != 0).any(): b.append("u_zero")
    return b
def reference(x, u, w):
    s = np.stack([mx_ref.matmul(mx_ref.quantize(u[r]), mx_ref.quantize(x[r]))[0] for r in range(N)]).reshape(-1) + np.float32(0.0)
    best = np.lexsort((np.arange(N * T), -s))[:K]
    V = mx_ref.quantize(cols(np.concatenate(list(x), axis=1), best))
    y = np.zeros((N, 128, O * K), np.float32)
    for r in range(N):
        for o in range(O): y[r][:, K * o:K * o + K] = mx_ref.matmul(mx_ref.quantize(np.ascontiguousarray(w[r][:, 512 * o:512 * o + 512])), V)
    who = np.stack([best // T, best % T]).astype(np.float32)
    return {"y": y, "id": np.stack([who] * N)}

@@ -1,0 +1,364 @@
+from concourse.bass import DstId, RemoteDMATransfer
+from concourse.mybir import dt, AluOpType, ActivationFunctionType
+
+K, O = 256, 4
+H = 256
+SCRATCH = {"ps": ("psum", [128, 4096], "float32")}
+
+
+def _bufs(dtype, **widths):
+    for name, n in widths.items():
+        SCRATCH[name] = ("sbuf", [128, n], dtype)
+
+
+_bufs("float8_e4m3fn_x4", cx=512, cu=128, cw=512, c1=512, c2=512)
+_bufs("uint8", sx=512, su=128, sw=512, s1=512, s2=512)
+_bufs("bfloat16", xb=2048, wb=2048, ub=16, up=512, neg=128, dm=128, fl=2048, cs=256, ce=512, f1=256, g1=128,
+      val=64, win=800, wt=544, z=136, zs=136, rz=136, iot=256, rep=1024, colr=1024, whow=512,
+      m0=6, m1=6, m2=6, m3=6, n0=16, n1=16, n2=16, n3=16)
+_bufs("float32", sc4=4, nd=4, th=512, pl=4, vb=64, hc=1, fx=1, fy=1, fz=1, fw=1, k16=16, k256=16, kb=2, rv=256,
+      h1=16, h2=16, h3=16, h4=16, k0=2, k1=2, k2=2, k3=2, sel=2, cp=1, t1=4, t2=4, t3=4,
+      cc=1, colw=512, idf=64, yy=2048, ysb=1024)
+_bufs("int32", ip=32, i3=32, i15=16, c16=16, c2i=16, ri=136, y17=1, a14=1, a112=1)
+_bufs("uint16", u4=32, pou=4, fo=2, fi=2, isl=16, r32=16, lst=16, q1=16, q1o=16, q2=16)
+SEMAPHORES = ["cv", "ca", "ct", "cp", "du", "dx0", "dx1", "dw", "dy0", "dy1", "did", "a1", "o1", "a2", "o2", "on", "ok", "om",
+              "an0", "an1", "an2", "an3", "ak0", "ak1", "ak2", "ak3", "am0", "am1", "am2", "am3"]
+STEP, TINY = 1.125 * 2.0 ** -24, 2.0 ** -124
+
+
+def rank_program(g, core, T, topo):
+    rank = T.rank_of(core)
+    if rank is None:
+        return
+    A, F = AluOpType, ActivationFunctionType
+    q = {"v": g.vector, "s": g.scalar, "t": g.tensor, "g": g, "y": g.sync}
+    cnt, seen = {}, {}
+
+    def inc(sem, ins, n=1):
+        ins.then_inc(T.sem[sem], n)
+        cnt[sem] = cnt.get(sem, 0) + n
+        return (sem, cnt[sem])
+
+    def wait(qn, *toks):
+        best = {}
+        for t in toks:
+            best[t[0]] = max(best.get(t[0], 0), t[1])
+        for sem, v in best.items():
+            if seen.get((qn, sem), 0) < v:
+                q[qn].wait_ge(T.sem[sem], v)
+                seen[(qn, sem)] = v
+
+    def vec(name, *args, after=()):
+        wait("v", *after)
+        calls = {"copy": g.vector.tensor_copy, "tt": g.vector.tensor_tensor, "ts": g.vector.tensor_scalar,
+                 "set": g.vector.memset, "scan": g.vector.tensor_tensor_scan, "tr": g.vector.transpose,
+                 "quant": g.vector.quantize_mx}
+        return inc("cv", calls[name](*args))
+
+    def act(out, in_, func, after=(), **kw):
+        wait("s", *after)
+        return inc("ca", g.scalar.activation(out, in_, func, **kw))
+
+    def mm(out, a, sa, b, sb, after=()):
+        wait("t", *after)
+        return inc("ct", g.tensor.matmul_mx(out, a, sa, b, sb, True, True))
+
+    mate, other = rank ^ 1, rank ^ 2
+    lower = rank < mate
+    a0 = 0 if lower else H
+    b0 = H - a0
+    f2 = 0 if rank < other else 1
+    k2 = 1 - f2
+    blk = 0 if lower else 1
+
+    du = inc("du", g.scalar.dma_start(T.ub[:, 0:4], T.u[:, 0:4]), 16)
+    dx = [inc("dx%d" % h, g.sync.dma_start(T.xb[:, 1024 * h:1024 * h + 1024], T.x[:, 1024 * h:1024 * h + 1024]), 16)
+          for h in (0, 1)]
+    dw = inc("dw", g.sync.dma_start(T.wb[:], T.w[:]), 16)
+
+    vneg = vec("set", T.neg[:], -1.0)
+    f = {"allow_small_or_imprecise_dtypes": True}
+    pip = inc("cp", g.iota(T.ip[:], [[0, 32]], 0, 1))
+    wait("g", vneg)
+    pdm = inc("cp", g.affine_select(T.dm[:], T.neg[:], [[-1, 128]], A.is_gt if lower else A.is_ge, 0.0, 0, 1))
+    pri = inc("cp", g.iota(T.ri[:], [[0, 17], [1, 8]], 0, 0))
+    pvb = inc("cp", g.iota(T.vb[:], [[128, 4], [1, 16]], 0, 0, **f))
+    pc16 = inc("cp", g.iota(T.c16[:], [[16, 16]], 0, 0))
+    pc2 = inc("cp", g.iota(T.c2i[:], [[1, 8], [0, 2]], 0, 0))
+    piot = inc("cp", g.iota(T.iot[:], [[1, 256]], -256, 0, **f))
+    pkb = inc("cp", g.iota(T.kb[:], [[128 if lower else -128, 2]], -256 if lower else -1, 1 if lower else -1, **f))
+    v = vec("ts", T.i3[:], T.ip[:], 3, None, A.bitwise_and, after=[pip])
+    vu4 = vec("copy", T.u4[:], T.i3[:], after=[v])
+    v15 = vec("ts", T.i15[:], T.ip[:, 0:16], 15, None, A.bitwise_and)
+    for out, bits in ((T.y17, 17), (T.a14, 14), (T.a112, 112)):
+        va = vec("ts", out[:], T.ip[:, 0:1], bits, None, A.bitwise_and)
+    w0 = 32 if lower else 32 + H
+    vwin = vec("set", T.win[:, w0 - 16:w0 + 272], 0.0)
+    s = act(T.up[:, 256:512], T.ub[:, 0:4].indirect(T.u4[:, 16:32]), F.Copy, after=[du, vu4])
+    v = vec("copy", T.up[:, 0:256], T.ub[:, 0:4].indirect(T.u4[:, 0:16]), after=[du, vu4])
+    vqu = vec("quant", T.cu[:], T.su[:], T.up[:], after=[v, s])
+    vec("tt", T.hc[:], T.ip[:, 0:1], T.i15[:, 0:1], A.subtract, after=[v15])
+    vec("ts", T.fx[:], T.y17[:], 1, 72.0, A.is_equal, A.mult, after=[va])
+    vec("ts", T.fy[:], T.y17[:], 16, 64.0, A.is_equal, A.mult)
+    vec("ts", T.fz[:], T.a14[:], 4.0, 7.0, A.mult, A.add)
+    vf = vec("ts", T.fw[:], T.a112[:], 0.5, 7.0, A.mult, A.add)
+
+    def constants():
+        vec("ts", T.fo[:, 0:1], T.fx[:], T.fy[:], T.fz[:], A.add, A.add, after=[vf])
+        vfo = vec("ts", T.fi[:, 0:1], T.fx[:], T.fy[:], T.fw[:], A.add, A.add)
+        vrz = vec("ts", T.rz[:], T.ri[:], 0, None, A.is_gt, after=[pri])
+        vval = vec("ts", T.val[:], T.vb[:], T.hc[:], -256.0, A.add, A.add, after=[pvb, vf])
+        return vfo, vrz, vval
+
+    def score_half(h, toks, row_first):
+        def row():
+            return mm(T.ps[:, 512 * h:512 * h + H], T.cu[:], T.su[:], T.cx[:, H * h:H * h + H], T.sx[:, H * h:H * h + H])
+
+        wait("t", *toks)
+        r = row() if row_first else None
+        for t in (2 * h, 2 * h + 1):
+            x = mm(T.ps[:, 512 * (2 + t):512 * (2 + t) + 128], T.cx[:, 128 * t:128 * t + 128],
+                   T.sx[:, 128 * t:128 * t + 128], T.cu[:], T.su[:])
+        return x, r or row()
+
+    def column(h, tx):
+        return act(T.sc4[:, 2 * h:2 * h + 2], T.ps[:, 512 * (2 + 2 * h):512 * (4 + 2 * h):512], F.Copy, after=[tx])
+
+    def inside(h, sc):
+        n = act(T.nd[:, 2 * h:2 * h + 2], T.ps[:, 512 * (2 + 2 * h):512 * (4 + 2 * h):512], F.Abs, scale=STEP, bias=TINY)
+        return [act(T.th[:, 128 * t:128 * t + 128], T.dm[:], F.Identity, after=[sc, n, pdm],
+                    scale=T.nd[:, t:t + 1], bias=T.sc4[:, t:t + 1]) for t in (2 * h, 2 * h + 1)]
+
+    def plain(t, j0, j1, at, toks=()):
+        p = 512 * (j0 // H) + j0 % H
+        if j1 <= 128 * t:
+            op = A.is_ge if lower else A.is_lt
+        else:
+            op = A.is_gt if lower else A.is_le
+        return vec("ts", T.fl[:, 512 * t + at:512 * t + at + j1 - j0], T.ps[:, p:p + j1 - j0], T.sc4[:, t:t + 1], None,
+                   op, after=toks)
+
+    def diag(t, at, tok):
+        p = 512 * (t // 2) + 128 * (t % 2)
+        return vec("tt", T.fl[:, 512 * t + at:512 * t + at + 128], T.ps[:, p:p + 128], T.th[:, 128 * t:128 * t + 128],
+                   A.is_gt if lower else A.is_le, after=[tok])
+
+    def total(t, i0, i1, tok):
+        fl = T.fl[:, 512 * t + i0:512 * t + i1]
+        return act(fl, fl, F.Copy, after=[tok], accum_out=T.pl[:, t:t + 1])
+
+    def halves(z, cs, j, tok):
+        return vec("scan", cs[:, j:j + 128], T.fl[:, z:z + 128], T.fl[:, z + 128:z + 256], 0.0, A.add, A.add, after=[tok])
+
+    def row_sum(t, tok):
+        z, j = 512 * t, 256 * (t // 2)
+        return vec("scan", T.ce[:, j:j + 256], T.fl[:, z:z + 256], T.fl[:, z + 256:z + 512], -256.0, A.add, A.add, after=[tok])
+
+    def cross(t, h, at, toks=()):
+        return plain(t, H * h, H * h + H, at, toks)
+
+    def places(f, k, sc, trk):
+        a = cross(2 * f, k, H, [trk])
+        b = cross(2 * f + 1, k, H)
+        th = inside(k, sc)
+        s0 = total(2 * f, 0, 512, a)
+        cross(2 * k, f, 0, [sc])
+        row_sum(2 * f + 1, b)
+        plain(2 * k, H * k + 128, H * k + 256, H + 128)
+        s1 = total(2 * k, 0, 512, diag(2 * k, H, th[0]))
+        t = 2 * k + 1
+        cross(t, f, 0)
+        plain(t, H * k, H * k + 128, H)
+        e = row_sum(t, diag(t, H + 128, th[1]))
+        vec("ts", T.pou[:, 1:4:2], T.ce[:, 255:512:256], 256.0, None, A.add, after=[e])
+        return vec("copy", T.pou[:, 0:4:2], T.pl[:, 0:4:2], after=[s0, s1])
+
+    def to_list(e, out, w0, w1, n):
+        e = vec("copy", T.win[:, 32:w1].indirect(T.pou[:]), T.val[:], after=[e, vval, vwin])
+        vec("tr", T.wt[:, 0:256], T.win[:, w0:w0 + 256], after=[e])
+        e = vec("tr", T.wt[:, 256:544], T.win[:, w0 - 16:w0 + 272])
+        runs = [(0, 128, 0, 0), (0, 64, 2, 1), (2, 64, 0, 1), *[(d, 32, d ^ 1, 2) for d in range(4)],
+                *[(d, 32, d ^ 3, 3) for d in range(4)]]
+        toks = []
+        for i, (d, m, src, j) in enumerate(runs):
+            ab = T.z[32 * d:32 * d + m, j:136:4], T.wt[32 * src:32 * src + m, 0:544:16]
+            toks.append(vec("copy", *ab, after=[e]) if i < 11 - n else act(*ab, F.Copy, after=[e]))
+        e = vec("scan", T.zs[:], T.rz[:], T.z[:], 0.0, A.mult, A.add, after=[*toks, vrz])
+        return e, vec("ts", out[:], T.zs[:].indirect(T.fo[:, 0:1]), 256.0, None, A.add, after=[e, vfo])
+
+    def pick(c_to, s_to, j, c, s, i0, i1, off, *toks):
+        v = vec("copy", c_to[:, j:j + K].bitcast(dt.uint32), c[:, i0:i1].bitcast(dt.uint32).indirect(off[:]), after=toks)
+        return v, act(s_to[:, j:j + K], s[:, i0:i1].indirect(off[:]), F.Copy, after=toks)
+
+    vq = vec("quant", T.cx[:, 0:H], T.sx[:, 0:H], T.xb[:, 0:1024], after=[dx[0]])
+    tx, tr0 = score_half(0, [vqu, vq], False)
+    sc0 = column(0, tx)
+    th0 = inside(0, sc0)
+    vfo, vrz, vval = constants()
+    vq = vec("quant", T.cx[:, H:2 * H], T.sx[:, H:2 * H], T.xb[:, 1024:2048], after=[dx[1]])
+    plain(0, 128, 256, 128, [sc0, tr0])
+    plain(1, 0, 128, 0)
+    diag(0, 0, th0[0])
+    diag(1, 128, th0[1])
+    tx, tr1 = score_half(1, [vq], True)
+    zl, ql = to_list(places(0, 1, column(1, tx), tr1), T.lst, w0, 544, 5)
+
+    def send(c, s, j, to, arr, out, pk):
+        rid, pid, _ = topo.addr(T.cores[to])
+        m, n = topo.mask(core, T.cores[to]), len(topo.engines(core, T.cores[to]))
+        wait("g", pk[0])
+        cc = c[:, j:j + K].bitcast(dt.uint8)
+        g.remote_dma(cc, cc, T.sem[arr], T.sem[out], pid, rid, m)
+        wait("g", pk[1])
+        g.remote_dma(s[:, j:j + K], s[:, j:j + K], T.sem[arr], T.sem[out], pid, rid, m)
+        return (arr, 2 * n), (out, 2 * n)
+
+    def tell(what, n, *toks):
+        tr, arr = [], {}
+        for i, r in enumerate((mate, other, other ^ 1)):
+            rid, pid, _ = topo.addr(T.cores[r])
+            eng = topo.engines(core, T.cores[r])[4 * i:4 * i + 4]
+            me = T["%s%d" % (what, rank)][:, 0:n]
+            tr.append(RemoteDMATransfer(dst_ids=[DstId(rid=rid, pnc=pid)], dma_engine_mask=sum(1 << e for e in eng),
+                                        remote_sem=T.sem["a%s%d" % (what, rank)], src=me, dst=me))
+            arr[r] = ("a%s%d" % (what, r), 4)
+        wait("g", *toks)
+        g.remote_dma_fused(tr, local_sem=T.sem["o" + what])
+        return arr, ("o" + what, 12)
+
+    snum = act(T["n%d" % rank][:, 0:8], T.zs[:, 7:64:8], F.Copy, after=[zl])
+    arrn, outn = tell("n", 8, snum)
+    p1 = pick(T.c1, T.s1, a0, T.cx, T.sx, 0, 512, T.lst, ql)
+    arr1, out1 = send(T.c1, T.s1, a0, mate, "a1", "o1", p1)
+    wait("t", *p1)
+    for t in (0, 1):
+        tx = mm(T.ps[:, 512 * (2 + t):512 * (2 + t) + 128], T.c1[:, a0 + 128 * t:a0 + 128 * t + 128],
+                T.s1[:, a0 + 128 * t:a0 + 128 * t + 128], T.cu[:], T.su[:])
+    sk = act(T["k%d" % rank][:, 0:2], T.ps[:, 1024:2048:512], F.Copy, after=[tx])
+    arrk, outk = tell("k", 2, sk)
+
+    vr32 = vec("copy", T.r32[:], T.c2i[:], after=[pc2])
+    vk16 = vec("tt", T.k16[:], T.i15[:], T.c16[:], A.add, after=[pc16])
+    vec("ts", T.k256[:], T.k16[:], -256.0, None, A.add, after=[vk16])
+    vm = vec("set", T["m%d" % rank][:], 0.0)
+    vw = vec("quant", T.cw[:], T.sw[:], T.wb[:], after=[dw])
+    vwin = vec("set", T.win[:, 16:304], 0.0)
+
+    def replicated(r):
+        return act(T.rep[:, 256 * r:256 * r + 256], T["n%d" % r][:, 0:8].indirect(T.r32[:]), F.Copy,
+                   after=[vr32, snum if r == rank else arrn[r]])
+
+    def turned(r, tok):
+        return vec("tr", T.colr[:, 256 * r:256 * r + 256], T.rep[:, 256 * r:256 * r + 256], after=[tok])
+
+    rp = {rank: replicated(rank)}
+    t = mm(T.ps[:, 0:256], T.cu[:], T.su[:], T.c1[:, a0:a0 + H], T.s1[:, a0:a0 + H])
+    srv = act(T.rv[:], T.ps[:, 0:256], F.Copy, after=[t])
+    for r in (mate, other):
+        rp[r] = replicated(r)
+    tu = {r: turned(r, rp[r]) for r in (rank, mate)}
+
+    def kk(r, t, n=1):
+        return T["k%d" % r][:, t:t + n]
+
+    vcp = vec("tt", T.cp[:], kk(other, blk), kk(other ^ 1, blk), A.max, after=[arrk[other], arrk[other ^ 1]])
+    vsel = vec("tt", T.sel[:], kk(rank, 0, 2), kk(mate, 0, 2), A.is_ge if lower else A.is_gt, after=[arrk[mate], sk])
+
+    def sides(at, row, *toks):
+        return act(T.fl[:, at:at + H], row, F.Sign, scale=-1.0, bias=T.cp[:], after=[vcp, *toks])
+
+    sides(0, T.rv[:], srv)
+
+    row = [mm(T.ps[:, b:b + H], T.cu[:], T.su[:], T.c1[:, b0:b0 + H], T.s1[:, b0:b0 + H], after=[arr1, sk]) for b in (512, 1024)]
+    theirs = T.ps[:, 512:768]
+    rows = (T.rv[:], theirs) if lower else (theirs, T.rv[:])
+    v = vec("tt", T.f1[:], rows[0], rows[1], A.is_ge, after=[row[0], srv])
+    mine = T.g1[:, 127:128]
+    vm1 = vec("scan", T.g1[:], T.f1[:, 0:128], T.f1[:, 128:256], -256.0, A.add, A.add, after=[v])
+
+    def choice(m, h1, h2, out, *toks):
+        v = vec("ts", h1[:], T.k256[:], m, 256.0, A.is_ge, A.mult, after=toks)
+        v = vec("tt", h2[:], T.k16[:], h1[:], A.add, after=[v])
+        return vec("copy", out[:], h2[:], after=[v])
+
+    vc = choice(mine, T.h1, T.h2, T.q1, vm1)
+    ss = sides(H, T.ps[:, 1024:1280], row[1])
+    p2 = pick(T.c2, T.s2, H * f2, T.c1, T.s1, 0, 512, T.q1, vc, arr1, *p1)
+
+    arr2, out2 = send(T.c2, T.s2, H * f2, other, "a2", "o2", p2)
+
+    msg = T["m%d" % rank]
+    sc = act(T.fl[:, 512:1024], T.fl[:, 0:512], F.Relu, scale=1.0 if f2 == 0 else -1.0, accum_out=T.cc[:], after=[ss])
+    smine = act(msg[:, 4:5], mine, F.Copy, after=[vm1, vm])
+    c = [vec("ts", T.fl[:, 1024 + H * i:1280 + H * i], theirs, kk(rank, i), None, A.is_gt if lower else A.is_ge)
+         for i in (0, 1)]
+    c = [halves(1024 + H * i, T.cs, 128 * i, c[i]) for i in (0, 1)]
+    for i in (0, 1):
+        at = 2 * f2 + i
+        vec("ts", msg[:, at:at + 1], T.cs[:, 128 * i + 127:128 * i + 128], T.kb[:, i:i + 1], T.sel[:, i:i + 1],
+            A.add, A.mult, after=[c[i], pkb, vsel, vm])
+    at, sign = 2 * k2 + blk, -1.0 if f2 == 0 else 1.0
+    vmsg = vec("ts", msg[:, at:at + 1], T.cc[:], sign, -256.0 * sign, A.mult, A.add, after=[sc])
+    arrm, outm = tell("m", 6, vmsg, smine)
+
+    def products(h, banks, toks):
+        return [mm(T.ps[:, 512 * b:512 * b + H], T.cw[:, 128 * o:128 * o + 128], T.sw[:, 128 * o:128 * o + 128],
+                   T.c2[:, H * h:H * h + H], T.s2[:, H * h:H * h + H], after=toks) for o, b in enumerate(banks)]
+
+    def result(h, o, b):
+        return T.yy[:, 512 * o + H * h:512 * o + H * h + H], T.ps[:, 512 * b:512 * b + H]
+
+    def col(h, lists, *toks):
+        return act(T.colw[:, H * h:H * h + H], T.colr[:, 512 * h:512 * h + 512].indirect(lists[:]), F.Identity, bias=256.0,
+                   after=toks)
+
+    def who(h, m, *toks):
+        return vec("ts", T.whow[:, H * h:H * h + H], T.iot[:], m, 2.0 * h, A.is_ge, A.add, after=[piot, *toks])
+
+    bf, bk = [4, 5, 6, 7], [2, 3, 0, 1]
+    typ = products(f2, bf, [vw, *p2])
+    vf = who(f2, mine)
+    tu[other] = turned(other, rp[other])
+    done = [act(*result(f2, o, bf[o]), F.Copy, after=[typ[o]]) for o in (0, 1)]
+    rp[other ^ 1] = replicated(other ^ 1)
+    done += [vec("copy", *result(f2, o, bf[o]), after=[typ[o]]) for o in (2, 3)]
+    tu[other ^ 1] = turned(other ^ 1, rp[other ^ 1])
+    sf = col(f2, T.q1, vc, tu[rank], tu[mate])
+    tyq = products(k2, bk, [arr2, sk, srv, vmsg, ss])
+
+    def m4(r):
+        return T["m%d" % r][:, 0:4]
+
+    def results(*os):
+        return [act(*result(k2, o, bk[o]), F.Copy, after=[tyq[o]]) for o in os]
+
+    there = results(0, 1)
+    v = vec("tt", T.t1[:], m4(rank), m4(mate), A.add, after=[vmsg, arrm[mate]])
+    v = vec("tt", T.t2[:], T.t1[:], m4(other), A.add, after=[v, arrm[other]])
+    v = vec("tt", T.t3[:], T.t2[:], m4(other ^ 1), A.add, after=[v, arrm[other ^ 1]])
+    v = vec("ts", T.pou[:], T.t3[:], 512.0, None, A.add, after=[v])
+    v2 = to_list(v, T.q2, 32, 800, 3)[1]
+    there += results(2, 3)
+
+    mo = T["m%d" % other][:, 4:5]
+    for o in range(O):
+        src, out = T.yy[:, 512 * o:512 * o + 512].indirect(T.q2[:]), T.ysb[:, K * o:K * o + K]
+        toks = [v2, done[o], there[o]]
+        tok = vec("copy", out, src, after=toks) if o % 2 == 0 else act(out, src, F.Copy, after=toks)
+        y = "s" if o == 3 else "y"
+        wait(y, tok)
+        inc("dy%d" % (o == 3), q[y].dma_start(T.y[:, K * o:K * o + K], out), 16)
+        if o == 0:
+            vo = choice(mo, T.h3, T.h4, T.q1o, arrm[other])
+            vk = who(k2, mo)
+            vs = vec("ts", T.isl[:], T.zs[:].indirect(T.fi[:, 0:1]), 256.0, None, A.add)
+        if o == 1:
+            so = col(k2, T.q1o, vo, tu[other], tu[other ^ 1])
+    ids = [vec("copy", T.idf[:, 0:32], T.whow[:].indirect(T.isl[:, 0:2]), after=[vs, vf, vk]),
+           vec("copy", T.idf[:, 32:64], T.colw[:].indirect(T.isl[:, 0:2]), after=[sf, so])]
+    for i in (0, 1):
+        wait("y", ids[i])
+        inc("did", g.sync.dma_start(T.id[i:i + 1, :], T.idf[0:128:16, 32 * i:32 * i + 32]), 16)
+
+    wait("g", out1, outn, outk, out2, outm, arr1, arr2, *arrn.values(), *arrk.values(), *arrm.values(),
+         *[(s, n) for s, n in cnt.items()])

@@ -11,18 +11,18 @@ def _bufs(dtype, **widths):
         SCRATCH[name] = ("sbuf", [128, n], dtype)
 
 
-_bufs("float8_e4m3fn_x4", cx=512, cu=128, cw=512, c1=512, c2=512)
-_bufs("uint8", sx=512, su=128, sw=512, s1=512, s2=512)
+_bufs("float8_e4m3fn_x4", cx=512, cu=128, cw=512, c1=512, c2=512, c3=256)
+_bufs("uint8", sx=512, su=128, sw=512, s1=512, s2=512, s3=256)
 _bufs("bfloat16", xb=2048, wb=2048, ub=16, up=512, neg=128, dm=128, fl=2048, cs=256, ce=512, f1=256, g1=128,
-      val=64, win=800, wt=544, z=136, zs=136, rz=136, iot=256, rep=1024, colr=1024, whow=512,
-      m0=6, m1=6, m2=6, m3=6, n0=16, n1=16, n2=16, n3=16)
-_bufs("float32", sc4=4, nd=4, th=512, pl=4, vb=64, hc=1, fx=1, fy=1, fz=1, fw=1, k16=16, k256=16, kb=2, rv=256,
-      h1=16, h2=16, h3=16, h4=16, k0=2, k1=2, k2=2, k3=2, sel=2, cp=1, t1=4, t2=4, t3=4,
-      cc=1, colw=512, idf=64, yy=2048, ysb=1024)
-_bufs("int32", ip=32, i3=32, i15=16, c16=16, c2i=16, ri=136, y17=1, a14=1, a112=1)
-_bufs("uint16", u4=32, pou=4, fo=2, fi=2, isl=16, r32=16, lst=16, q1=16, q1o=16, q2=16)
-SEMAPHORES = ["cv", "ca", "ct", "cp", "du", "dx0", "dx1", "dw", "dy0", "dy1", "did", "a1", "o1", "a2", "o2", "on", "ok", "om",
-              "an0", "an1", "an2", "an3", "ak0", "ak1", "ak2", "ak3", "am0", "am1", "am2", "am3"]
+      val=64, val2=64, win=800, wt=544, z=136, zs=136, rz=136, iot=256, rep=512, colr=512, whow=512,
+      nme=8, nth=8, pme=16, pth=16)
+_bufs("float32", sc4=4, nd=4, th=512, pl=4, vb=64, vb2=64, hc=1, hc2=1, fx=1, fy=1, fz=1, fw=1, k16=16, k256=16, kb=2,
+      k32=8, rv=256, rows=512, sg=32, sgt=32, h1=16, h2=16, dn=8, h3=8, h4=8, k0=2, k1=2, k2=2, k3=2, m0=4, m1=4, m2=4,
+      m3=4, lose=2, cp=2, t1=4, idf=64, ysb=1024)
+_bufs("int32", ip=32, i3=32, i15=16, c16=16, c2i=16, ri=136, y17=1, a14=1, a112=1, a96=8, kb0=2, k320=8)
+_bufs("uint16", u4=32, pou=4, fo=2, r32=16, lst=32, q1=16, q2=32)
+SEMAPHORES = ["cv", "ca", "ct", "cp", "du", "dx0", "dx1", "dw", "dy0", "dy1", "a1", "o1", "a2", "o2", "on", "ok", "om", "op",
+              "an", "ap", "ak0", "ak1", "ak2", "ak3", "am0", "am1", "am2", "am3"]
 STEP, TINY = 1.125 * 2.0 ** -24, 2.0 ** -124
 
 
@@ -69,7 +69,6 @@ def rank_program(g, core, T, topo):
     b0 = H - a0
     f2 = 0 if rank < other else 1
     k2 = 1 - f2
-    blk = 0 if lower else 1
 
     du = inc("du", g.scalar.dma_start(T.ub[:, 0:4], T.u[:, 0:4]), 16)
     dx = [inc("dx%d" % h, g.sync.dma_start(T.xb[:, 1024 * h:1024 * h + 1024], T.x[:, 1024 * h:1024 * h + 1024]), 16)
@@ -86,7 +85,9 @@ def rank_program(g, core, T, topo):
     pc16 = inc("cp", g.iota(T.c16[:], [[16, 16]], 0, 0))
     pc2 = inc("cp", g.iota(T.c2i[:], [[1, 8], [0, 2]], 0, 0))
     piot = inc("cp", g.iota(T.iot[:], [[1, 256]], -256, 0, **f))
-    pkb = inc("cp", g.iota(T.kb[:], [[128 if lower else -128, 2]], -256 if lower else -1, 1 if lower else -1, **f))
+    inc("cp", g.iota(T.kb0[:], [[-32 if lower else 32, 2]], 255 if lower else 0, -1 if lower else 1))
+    inc("cp", g.iota(T.k320[:], [[32, 8]], -256, 1))
+    pvb2 = inc("cp", g.iota(T.vb2[:], [[256, 2], [32, 2], [1, 16]], -256, 0, **f))
     v = vec("ts", T.i3[:], T.ip[:], 3, None, A.bitwise_and, after=[pip])
     vu4 = vec("copy", T.u4[:], T.i3[:], after=[v])
     v15 = vec("ts", T.i15[:], T.ip[:, 0:16], 15, None, A.bitwise_and)
@@ -105,7 +106,7 @@ def rank_program(g, core, T, topo):
 
     def constants():
         vec("ts", T.fo[:, 0:1], T.fx[:], T.fy[:], T.fz[:], A.add, A.add, after=[vf])
-        vfo = vec("ts", T.fi[:, 0:1], T.fx[:], T.fy[:], T.fw[:], A.add, A.add)
+        vfo = vec("ts", T.fo[:, 1:2], T.fx[:], T.fy[:], T.fw[:], A.add, A.add)
         vrz = vec("ts", T.rz[:], T.ri[:], 0, None, A.is_gt, after=[pri])
         vval = vec("ts", T.val[:], T.vb[:], T.hc[:], -256.0, A.add, A.add, after=[pvb, vf])
         return vfo, vrz, vval
@@ -173,8 +174,8 @@ def rank_program(g, core, T, topo):
         vec("ts", T.pou[:, 1:4:2], T.ce[:, 255:512:256], 256.0, None, A.add, after=[e])
         return vec("copy", T.pou[:, 0:4:2], T.pl[:, 0:4:2], after=[s0, s1])
 
-    def to_list(e, out, w0, w1, n):
-        e = vec("copy", T.win[:, 32:w1].indirect(T.pou[:]), T.val[:], after=[e, vval, vwin])
+    def to_list(e, val, out, w0, w1, n):
+        e = vec("copy", T.win[:, 32:w1].indirect(T.pou[:]), val[:], after=[e, vval, vwin])
         vec("tr", T.wt[:, 0:256], T.win[:, w0:w0 + 256], after=[e])
         e = vec("tr", T.wt[:, 256:544], T.win[:, w0 - 16:w0 + 272])
         runs = [(0, 128, 0, 0), (0, 64, 2, 1), (2, 64, 0, 1), *[(d, 32, d ^ 1, 2) for d in range(4)],
@@ -184,11 +185,11 @@ def rank_program(g, core, T, topo):
             ab = T.z[32 * d:32 * d + m, j:136:4], T.wt[32 * src:32 * src + m, 0:544:16]
             toks.append(vec("copy", *ab, after=[e]) if i < 11 - n else act(*ab, F.Copy, after=[e]))
         e = vec("scan", T.zs[:], T.rz[:], T.z[:], 0.0, A.mult, A.add, after=[*toks, vrz])
-        return e, vec("ts", out[:], T.zs[:].indirect(T.fo[:, 0:1]), 256.0, None, A.add, after=[e, vfo])
+        return e, vec("ts", out[:], T.zs[:].indirect(T.fo[:, 0:2]), 256.0, None, A.add, after=[e, vfo])
 
-    def pick(c_to, s_to, j, c, s, i0, i1, off, *toks):
-        v = vec("copy", c_to[:, j:j + K].bitcast(dt.uint32), c[:, i0:i1].bitcast(dt.uint32).indirect(off[:]), after=toks)
-        return v, act(s_to[:, j:j + K], s[:, i0:i1].indirect(off[:]), F.Copy, after=toks)
+    def pick(c_to, s_to, j, c, s, off, *toks):
+        v = vec("copy", c_to[:, j:j + K].bitcast(dt.uint32), c[:].bitcast(dt.uint32).indirect(off[:, 0:16]), after=toks)
+        return v, act(s_to[:, j:j + K], s[:].indirect(off[:, 0:16]), F.Copy, after=toks)
 
     vq = vec("quant", T.cx[:, 0:H], T.sx[:, 0:H], T.xb[:, 0:1024], after=[dx[0]])
     tx, tr0 = score_half(0, [vqu, vq], False)
@@ -201,7 +202,10 @@ def rank_program(g, core, T, topo):
     diag(0, 0, th0[0])
     diag(1, 128, th0[1])
     tx, tr1 = score_half(1, [vq], True)
-    zl, ql = to_list(places(0, 1, column(1, tx), tr1), T.lst, w0, 544, 5)
+    tall = mm(T.ps[:, 3072:3584], T.cu[:], T.su[:], T.cx[:], T.sx[:])
+    vpl = places(0, 1, column(1, tx), tr1)
+    srows = act(T.rows[:], T.ps[:, 3072:3584], F.Copy, after=[tall])
+    zl, ql = to_list(vpl, T.val, T.lst, w0, 544, 5)
 
     def send(c, s, j, to, arr, out, pk):
         rid, pid, _ = topo.addr(T.cores[to])
@@ -213,152 +217,133 @@ def rank_program(g, core, T, topo):
         g.remote_dma(s[:, j:j + K], s[:, j:j + K], T.sem[arr], T.sem[out], pid, rid, m)
         return (arr, 2 * n), (out, 2 * n)
 
-    def tell(what, n, *toks):
+    def note(dst, src, to, what, *toks):
+        rid, pid, _ = topo.addr(T.cores[to])
+        wait("g", *toks)
+        g.remote_dma(dst, src, T.sem["a" + what], T.sem["o" + what], pid, rid,
+                     sum(1 << e for e in topo.engines(core, T.cores[to])[0:8]))
+        return ("a" + what, 8), ("o" + what, 8)
+
+    def tell(what, me, *toks):
         tr, arr = [], {}
-        for i, r in enumerate((mate, other, other ^ 1)):
+        for r, e0, n in ((mate, 0, 8), (other, 8, 4), (other ^ 1, 12, 4)):
             rid, pid, _ = topo.addr(T.cores[r])
-            eng = topo.engines(core, T.cores[r])[4 * i:4 * i + 4]
-            me = T["%s%d" % (what, rank)][:, 0:n]
+            eng = topo.engines(core, T.cores[r])[e0:e0 + n]
             tr.append(RemoteDMATransfer(dst_ids=[DstId(rid=rid, pnc=pid)], dma_engine_mask=sum(1 << e for e in eng),
-                                        remote_sem=T.sem["a%s%d" % (what, rank)], src=me, dst=me))
-            arr[r] = ("a%s%d" % (what, r), 4)
+                                        remote_sem=T.sem["a%s%d" % (what, rank)], src=me, dst=T["%s%d" % (what, rank)][:]))
+            arr[r] = ("a%s%d" % (what, r), n)
         wait("g", *toks)
         g.remote_dma_fused(tr, local_sem=T.sem["o" + what])
-        return arr, ("o" + what, 12)
+        return arr, ("o" + what, 16)
 
-    snum = act(T["n%d" % rank][:, 0:8], T.zs[:, 7:64:8], F.Copy, after=[zl])
-    arrn, outn = tell("n", 8, snum)
-    p1 = pick(T.c1, T.s1, a0, T.cx, T.sx, 0, 512, T.lst, ql)
+    snum = act(T.nme[:], T.zs[:, 7:64:8], F.Copy, after=[zl])
+    arrn, outn = note(T.nth[:], T.nme[:], mate, "n", snum)
+    v = vec("copy", T.sg[:], T.rows[:].indirect(T.lst[:, 16:18]), after=[ql, srows])
+    vk = vec("tr", T.sgt[:], T.sg[:], after=[v])
+    kme = T.sgt[:, 15:17]
+    arrk, outk = tell("k", kme, vk)
+
+    p1 = pick(T.c1, T.s1, a0, T.cx, T.sx, T.lst, ql)
     arr1, out1 = send(T.c1, T.s1, a0, mate, "a1", "o1", p1)
-    wait("t", *p1)
-    for t in (0, 1):
-        tx = mm(T.ps[:, 512 * (2 + t):512 * (2 + t) + 128], T.c1[:, a0 + 128 * t:a0 + 128 * t + 128],
-                T.s1[:, a0 + 128 * t:a0 + 128 * t + 128], T.cu[:], T.su[:])
-    sk = act(T["k%d" % rank][:, 0:2], T.ps[:, 1024:2048:512], F.Copy, after=[tx])
-    arrk, outk = tell("k", 2, sk)
 
+    t = mm(T.ps[:, 0:256], T.cu[:], T.su[:], T.c1[:, a0:a0 + H], T.s1[:, a0:a0 + H], after=p1)
+    srv = act(T.rv[:], T.ps[:, 0:256], F.Copy, after=[t])
+    v = vec("ts", T.a96[:], T.ip[:, 0:8], 96, None, A.bitwise_and)
     vr32 = vec("copy", T.r32[:], T.c2i[:], after=[pc2])
     vk16 = vec("tt", T.k16[:], T.i15[:], T.c16[:], A.add, after=[pc16])
+    vec("tt", T.kb[:], T.kb0[:], T.a96[:, 0:2], A.subtract if lower else A.add, after=[v, pvb2])
+    vec("tt", T.k32[:], T.k320[:], T.a96[:], A.subtract)
+    v = vec("tt", T.hc2[:], T.a112[:], T.a96[:, 0:1], A.add)
     vec("ts", T.k256[:], T.k16[:], -256.0, None, A.add, after=[vk16])
-    vm = vec("set", T["m%d" % rank][:], 0.0)
+    vec("ts", T.val2[:], T.vb2[:], T.hc2[:], None, A.add, after=[v])
     vw = vec("quant", T.cw[:], T.sw[:], T.wb[:], after=[dw])
     vwin = vec("set", T.win[:, 16:304], 0.0)
 
-    def replicated(r):
-        return act(T.rep[:, 256 * r:256 * r + 256], T["n%d" % r][:, 0:8].indirect(T.r32[:]), F.Copy,
-                   after=[vr32, snum if r == rank else arrn[r]])
-
-    def turned(r, tok):
-        return vec("tr", T.colr[:, 256 * r:256 * r + 256], T.rep[:, 256 * r:256 * r + 256], after=[tok])
-
-    rp = {rank: replicated(rank)}
-    t = mm(T.ps[:, 0:256], T.cu[:], T.su[:], T.c1[:, a0:a0 + H], T.s1[:, a0:a0 + H])
-    srv = act(T.rv[:], T.ps[:, 0:256], F.Copy, after=[t])
-    for r in (mate, other):
-        rp[r] = replicated(r)
-    tu = {r: turned(r, rp[r]) for r in (rank, mate)}
-
-    def kk(r, t, n=1):
-        return T["k%d" % r][:, t:t + n]
-
-    vcp = vec("tt", T.cp[:], kk(other, blk), kk(other ^ 1, blk), A.max, after=[arrk[other], arrk[other ^ 1]])
-    vsel = vec("tt", T.sel[:], kk(rank, 0, 2), kk(mate, 0, 2), A.is_ge if lower else A.is_gt, after=[arrk[mate], sk])
-
-    def sides(at, row, *toks):
-        return act(T.fl[:, at:at + H], row, F.Sign, scale=-1.0, bias=T.cp[:], after=[vcp, *toks])
-
-    sides(0, T.rv[:], srv)
-
-    row = [mm(T.ps[:, b:b + H], T.cu[:], T.su[:], T.c1[:, b0:b0 + H], T.s1[:, b0:b0 + H], after=[arr1, sk]) for b in (512, 1024)]
-    theirs = T.ps[:, 512:768]
-    rows = (T.rv[:], theirs) if lower else (theirs, T.rv[:])
-    v = vec("tt", T.f1[:], rows[0], rows[1], A.is_ge, after=[row[0], srv])
-    mine = T.g1[:, 127:128]
-    vm1 = vec("scan", T.g1[:], T.f1[:, 0:128], T.f1[:, 128:256], -256.0, A.add, A.add, after=[v])
-
-    def choice(m, h1, h2, out, *toks):
-        v = vec("ts", h1[:], T.k256[:], m, 256.0, A.is_ge, A.mult, after=toks)
-        v = vec("tt", h2[:], T.k16[:], h1[:], A.add, after=[v])
-        return vec("copy", out[:], h2[:], after=[v])
-
-    vc = choice(mine, T.h1, T.h2, T.q1, vm1)
-    ss = sides(H, T.ps[:, 1024:1280], row[1])
-    p2 = pick(T.c2, T.s2, H * f2, T.c1, T.s1, 0, 512, T.q1, vc, arr1, *p1)
-
-    arr2, out2 = send(T.c2, T.s2, H * f2, other, "a2", "o2", p2)
+    def kk(r):
+        return T["k%d" % r]
 
     msg = T["m%d" % rank]
-    sc = act(T.fl[:, 512:1024], T.fl[:, 0:512], F.Relu, scale=1.0 if f2 == 0 else -1.0, accum_out=T.cc[:], after=[ss])
-    smine = act(msg[:, 4:5], mine, F.Copy, after=[vm1, vm])
-    c = [vec("ts", T.fl[:, 1024 + H * i:1280 + H * i], theirs, kk(rank, i), None, A.is_gt if lower else A.is_ge)
-         for i in (0, 1)]
+    vcp = vec("tt", T.cp[:], kk(other)[:], kk(other ^ 1)[:], A.max, after=[arrk[other], arrk[other ^ 1]])
+    s = [act(T.fl[:, H * i:H * i + H], T.rv[:], F.Sign, scale=-1.0, bias=T.cp[:, i:i + 1], after=[vcp, srv]) for i in (0, 1)]
+    how = (F.Sign, 1.0) if f2 == 0 else (F.Relu, 0.0)
+    smsg = [act(T.fl[:, 512 + H * i:768 + H * i], T.fl[:, H * i:H * i + H], how[0], scale=-1.0, bias=how[1],
+                accum_out=msg[:, 2 * k2 + i:2 * k2 + i + 1], after=[s[i]]) for i in (0, 1)]
+    c = [vec("ts", T.fl[:, 1024 + H * i:1280 + H * i], T.rv[:], kk(mate)[:, i:i + 1], None, A.is_ge if lower else A.is_gt,
+             after=[arrk[mate], srv]) for i in (0, 1)]
+    vl = vec("tt", T.lose[:], kme, kk(mate)[:], A.is_lt if lower else A.is_le)
     c = [halves(1024 + H * i, T.cs, 128 * i, c[i]) for i in (0, 1)]
     for i in (0, 1):
         at = 2 * f2 + i
-        vec("ts", msg[:, at:at + 1], T.cs[:, 128 * i + 127:128 * i + 128], T.kb[:, i:i + 1], T.sel[:, i:i + 1],
-            A.add, A.mult, after=[c[i], pkb, vsel, vm])
-    at, sign = 2 * k2 + blk, -1.0 if f2 == 0 else 1.0
-    vmsg = vec("ts", msg[:, at:at + 1], T.cc[:], sign, -256.0 * sign, A.mult, A.add, after=[sc])
-    arrm, outm = tell("m", 6, vmsg, smine)
+        vmsg = vec("ts", msg[:, at:at + 1], T.cs[:, 128 * i + 127:128 * i + 128], T.kb[:, i:i + 1], T.lose[:, i:i + 1],
+                   A.add, A.mult, after=[c[i], vl])
+    arrm, outm = tell("m", msg[:], vmsg, *smsg)
 
-    def products(h, banks, toks):
-        return [mm(T.ps[:, 512 * b:512 * b + H], T.cw[:, 128 * o:128 * o + 128], T.sw[:, 128 * o:128 * o + 128],
-                   T.c2[:, H * h:H * h + H], T.s2[:, H * h:H * h + H], after=toks) for o, b in enumerate(banks)]
+    row = mm(T.ps[:, 512:768], T.cu[:], T.su[:], T.c1[:, b0:b0 + H], T.s1[:, b0:b0 + H], after=[arr1])
+    theirs = T.ps[:, 512:768]
+    rows = (T.rv[:], theirs) if lower else (theirs, T.rv[:])
+    v = vec("tt", T.f1[:], rows[0], rows[1], A.is_ge, after=[row])
+    mine = T.g1[:, 127:128]
+    vm1 = vec("scan", T.g1[:], T.f1[:, 0:128], T.f1[:, 128:256], -256.0, A.add, A.add, after=[v])
+    nl, nu = (T.nme, T.nth) if lower else (T.nth, T.nme)
+    vdn = vec("tt", T.dn[:], nu[:], nl[:], A.subtract, after=[arrn, snum])
+    v = vec("ts", T.h1[:], T.k256[:], mine, 256.0, A.is_ge, A.mult, after=[vm1])
+    vh = vec("ts", T.h3[:], T.k32[:], mine, None, A.is_ge)
+    v = vec("tt", T.h2[:], T.k16[:], T.h1[:], A.add, after=[v])
+    vh = vec("tt", T.h4[:], T.h3[:], T.dn[:], A.mult, after=[vh, vdn])
+    vc = vec("copy", T.q1[:], T.h2[:], after=[v])
+    vpn = vec("tt", T.pme[:, 0:8], T.h4[:], nl[:], A.add, after=[vh])
+    p2 = pick(T.c2, T.s2, H * f2, T.c1, T.s1, T.q1, vc, arr1, *p1)
+    spn = act(T.pme[:, 8:9], mine, F.Copy, after=[vm1])
 
-    def result(h, o, b):
-        return T.yy[:, 512 * o + H * h:512 * o + H * h + H], T.ps[:, 512 * b:512 * b + H]
+    arr2, out2 = send(T.c2, T.s2, H * f2, other, "a2", "o2", p2)
+    arrp, outp = note(T.pth[:, 0:9], T.pme[:, 0:9], other, "p", vpn, spn)
 
-    def col(h, lists, *toks):
-        return act(T.colw[:, H * h:H * h + H], T.colr[:, 512 * h:512 * h + 512].indirect(lists[:]), F.Identity, bias=256.0,
-                   after=toks)
+    def replicated(h, src, *toks):
+        return act(T.rep[:, H * h:H * h + H], src[:, 0:8].indirect(T.r32[:]), F.Copy, after=[vr32, *toks])
+
+    def turned(h, tok):
+        return vec("tr", T.colr[:, H * h:H * h + H], T.rep[:, H * h:H * h + H], after=[tok])
 
     def who(h, m, *toks):
         return vec("ts", T.whow[:, H * h:H * h + H], T.iot[:], m, 2.0 * h, A.is_ge, A.add, after=[piot, *toks])
 
-    bf, bk = [4, 5, 6, 7], [2, 3, 0, 1]
-    typ = products(f2, bf, [vw, *p2])
-    vf = who(f2, mine)
-    tu[other] = turned(other, rp[other])
-    done = [act(*result(f2, o, bf[o]), F.Copy, after=[typ[o]]) for o in (0, 1)]
-    rp[other ^ 1] = replicated(other ^ 1)
-    done += [vec("copy", *result(f2, o, bf[o]), after=[typ[o]]) for o in (2, 3)]
-    tu[other ^ 1] = turned(other ^ 1, rp[other ^ 1])
-    sf = col(f2, T.q1, vc, tu[rank], tu[mate])
-    tyq = products(k2, bk, [arr2, sk, srv, vmsg, ss])
+    s = replicated(f2, T.pme, vpn)
+    who(f2, mine)
+    turned(f2, s)
 
-    def m4(r):
-        return T["m%d" % r][:, 0:4]
+    v = vec("tt", T.t1[:], msg[:], T["m%d" % mate][:], A.add, after=[*smsg, arrm[mate]])
+    for i in range(4):
+        e = vec("ts", T.pou[:, i:i + 1], T.t1[:, i:i + 1], T["m%d" % other][:, i:i + 1], T["m%d" % (other ^ 1)][:, i:i + 1],
+                A.add, A.add, after=[v, arrm[other], arrm[other ^ 1]])
+    v2 = to_list(e, T.val2, T.q2, 32, 800, 5)[1]
 
-    def results(*os):
-        return [act(*result(k2, o, bk[o]), F.Copy, after=[tyq[o]]) for o in os]
+    p3 = pick(T.c3, T.s3, 0, T.c2, T.s2, T.q2, v2, arr2, *p2)
+    ty = [mm(T.ps[:, 512 * (4 + o):512 * (4 + o) + K], T.cw[:, 128 * o:128 * o + 128], T.sw[:, 128 * o:128 * o + 128],
+             T.c3[:], T.s3[:], after=[vw, *p3]) for o in range(O)]
+    s = replicated(k2, T.pth, arrp)
+    vw2 = who(k2, T.pth[:, 8:9], arrp)
+    ids = [vec("copy", T.idf[:, 0:32], T.whow[:].indirect(T.q2[:, 16:18]), after=[vw2])]
 
-    there = results(0, 1)
-    v = vec("tt", T.t1[:], m4(rank), m4(mate), A.add, after=[vmsg, arrm[mate]])
-    v = vec("tt", T.t2[:], T.t1[:], m4(other), A.add, after=[v, arrm[other]])
-    v = vec("tt", T.t3[:], T.t2[:], m4(other ^ 1), A.add, after=[v, arrm[other ^ 1]])
-    v = vec("ts", T.pou[:], T.t3[:], 512.0, None, A.add, after=[v])
-    v2 = to_list(v, T.q2, 32, 800, 3)[1]
-    there += results(2, 3)
-
-    mo = T["m%d" % other][:, 4:5]
-    for o in range(O):
-        src, out = T.yy[:, 512 * o:512 * o + 512].indirect(T.q2[:]), T.ysb[:, K * o:K * o + K]
-        toks = [v2, done[o], there[o]]
-        tok = vec("copy", out, src, after=toks) if o % 2 == 0 else act(out, src, F.Copy, after=toks)
-        y = "s" if o == 3 else "y"
+    def store(y, out, in_, tok):
         wait(y, tok)
-        inc("dy%d" % (o == 3), q[y].dma_start(T.y[:, K * o:K * o + K], out), 16)
-        if o == 0:
-            vo = choice(mo, T.h3, T.h4, T.q1o, arrm[other])
-            vk = who(k2, mo)
-            vs = vec("ts", T.isl[:], T.zs[:].indirect(T.fi[:, 0:1]), 256.0, None, A.add)
-        if o == 1:
-            so = col(k2, T.q1o, vo, tu[other], tu[other ^ 1])
-    ids = [vec("copy", T.idf[:, 0:32], T.whow[:].indirect(T.isl[:, 0:2]), after=[vs, vf, vk]),
-           vec("copy", T.idf[:, 32:64], T.colw[:].indirect(T.isl[:, 0:2]), after=[sf, so])]
-    for i in (0, 1):
-        wait("y", ids[i])
-        inc("did", g.sync.dma_start(T.id[i:i + 1, :], T.idf[0:128:16, 32 * i:32 * i + 32]), 16)
+        inc("dy%d" % (y == "s"), q[y].dma_start(out, in_), 16)
 
-    wait("g", out1, outn, outk, out2, outm, arr1, arr2, *arrn.values(), *arrk.values(), *arrm.values(),
+    def result(o):
+        ab = T.ysb[:, K * o:K * o + K], T.ps[:, 512 * (4 + o):512 * (4 + o) + K]
+        return vec("copy", *ab, after=[ty[o]]) if o % 2 == 0 else act(*ab, F.Copy, after=[ty[o]])
+
+    def store_y(y, o, tok):
+        store(y, T.y[:, K * o:K * o + K], T.ysb[:, K * o:K * o + K], tok)
+
+    store("y", T.id[0:1, :], T.idf[0:128:16, 0:32], ids[0])
+    store_y("y", 0, result(0))
+    v = turned(k2, s)
+    store_y("y", 1, result(1))
+    r2 = result(2)
+    ids.append(vec("ts", T.idf[:, 32:64], T.colr[:].indirect(T.q2[:, 16:18]), 256.0, None, A.add, after=[v]))
+    store_y("s", 3, result(3))
+    store_y("y", 2, r2)
+    store("s", T.id[1:2, :], T.idf[0:128:16, 32:64], ids[1])
+
+    wait("g", out1, outn, outk, out2, outm, outp, arr1, arr2, arrn, arrp, *arrk.values(), *arrm.values(),
          *[(s, n) for s, n in cnt.items()])

@@ -11,16 +11,16 @@ def _bufs(dtype, **widths):
         SCRATCH[name] = ("sbuf", [128, n], dtype)
 
 
-_bufs("float8_e4m3fn_x4", cx=512, cu=128, cw=512, c1=512, c2=512, c3=256)
-_bufs("uint8", sx=512, su=128, sw=512, s1=512, s2=512, s3=256)
-_bufs("bfloat16", xb=2048, wb=2048, ub=16, up=512, neg=128, dm=128, fl=2048, cs=256, ce=512, f1=256, g1=128,
+_bufs("float8_e4m3fn_x4", cx=512, cq=128, cu=128, cw=512, c1=512, c2=512, c3=256)
+_bufs("uint8", sx=512, sq=128, su=128, sw=512, s1=512, s2=512, s3=256)
+_bufs("bfloat16", xb=2048, wb=2048, up=512, neg=128, dm=128, fl=2048, cs=256, ce=512, f1=256, g1=128,
       val=64, val2=64, win=800, wt=544, z=136, zs=136, rz=136, iot=256, rep=512, colr=512, whow=512,
       nme=8, nth=8, pme=16, pth=16)
 _bufs("float32", sc4=4, nd=4, th=512, pl=4, vb=64, vb2=64, hc=1, hc2=1, fx=1, fy=1, fz=1, fw=1, k16=16, k256=16, kb=2,
       k32=8, rv=256, rows=512, sg=32, sgt=32, h1=16, h2=16, dn=8, h3=8, h4=8, k0=2, k1=2, k2=2, k3=2, m0=4, m1=4, m2=4,
       m3=4, lose=2, cp=2, t1=4, idf=64, ysb=1024)
-_bufs("int32", ip=32, i3=32, i15=16, c16=16, c2i=16, ri=136, y17=1, a14=1, a112=1, a96=8, kb0=2, k320=8)
-_bufs("uint16", u4=32, pou=4, fo=2, r32=16, lst=32, q1=16, q2=32)
+_bufs("int32", ip=16, i15=16, c16=16, c2i=16, y17=1, a14=1, a112=1, a96=8, kb0=2, k320=8)
+_bufs("uint16", u0=8, pou=4, fo=2, r32=16, lst=32, q1=16, q2=32)
 SEMAPHORES = ["cv", "ca", "ct", "cp", "du", "dx0", "dx1", "dw", "dy0", "dy1", "a1", "o1", "a2", "o2", "on", "ok", "om", "op",
               "an", "ap", "ak0", "ak1", "ak2", "ak3", "am0", "am1", "am2", "am3"]
 STEP, TINY = 1.125 * 2.0 ** -24, 2.0 ** -124
@@ -70,65 +70,71 @@ def rank_program(g, core, T, topo):
     f2 = 0 if rank < other else 1
     k2 = 1 - f2
 
-    du = inc("du", g.scalar.dma_start(T.ub[:, 0:4], T.u[:, 0:4]), 16)
+    du = inc("du", g.scalar.dma_start(T.up[:, 0:8], T.u[:, 0:8]), 16)
     dx = [inc("dx%d" % h, g.sync.dma_start(T.xb[:, 1024 * h:1024 * h + 1024], T.x[:, 1024 * h:1024 * h + 1024]), 16)
           for h in (0, 1)]
     dw = inc("dw", g.sync.dma_start(T.wb[:], T.w[:]), 16)
 
     vneg = vec("set", T.neg[:], -1.0)
     f = {"allow_small_or_imprecise_dtypes": True}
-    pip = inc("cp", g.iota(T.ip[:], [[0, 32]], 0, 1))
+    pip = inc("cp", g.iota(T.ip[:], [[0, 16]], 0, 1))
+    pvb = inc("cp", g.iota(T.vb[:], [[128, 4], [1, 16]], 0, 0, **f))
     wait("g", vneg)
     pdm = inc("cp", g.affine_select(T.dm[:], T.neg[:], [[-1, 128]], A.is_gt if lower else A.is_ge, 0.0, 0, 1))
-    pri = inc("cp", g.iota(T.ri[:], [[0, 17], [1, 8]], 0, 0))
-    pvb = inc("cp", g.iota(T.vb[:], [[128, 4], [1, 16]], 0, 0, **f))
     pc16 = inc("cp", g.iota(T.c16[:], [[16, 16]], 0, 0))
     pc2 = inc("cp", g.iota(T.c2i[:], [[1, 8], [0, 2]], 0, 0))
     piot = inc("cp", g.iota(T.iot[:], [[1, 256]], -256, 0, **f))
     inc("cp", g.iota(T.kb0[:], [[-32 if lower else 32, 2]], 255 if lower else 0, -1 if lower else 1))
     inc("cp", g.iota(T.k320[:], [[32, 8]], -256, 1))
     pvb2 = inc("cp", g.iota(T.vb2[:], [[256, 2], [32, 2], [1, 16]], -256, 0, **f))
-    v = vec("ts", T.i3[:], T.ip[:], 3, None, A.bitwise_and, after=[pip])
-    vu4 = vec("copy", T.u4[:], T.i3[:], after=[v])
-    v15 = vec("ts", T.i15[:], T.ip[:, 0:16], 15, None, A.bitwise_and)
+    w0 = 32 if lower else 32 + H
+    vec("set", T.up[:, 8:512], 0.0)
+    vec("set", T.u0[:], 0)
+    v1 = vec("set", T.rz[:], 1.0)
+    vwin = vec("set", T.win[:, w0 - 16:w0 + 272], 0.0)
+    v15 = vec("ts", T.i15[:], T.ip[:], 15, None, A.bitwise_and, after=[pip])
     for out, bits in ((T.y17, 17), (T.a14, 14), (T.a112, 112)):
         va = vec("ts", out[:], T.ip[:, 0:1], bits, None, A.bitwise_and)
-    w0 = 32 if lower else 32 + H
-    vwin = vec("set", T.win[:, w0 - 16:w0 + 272], 0.0)
-    s = act(T.up[:, 256:512], T.ub[:, 0:4].indirect(T.u4[:, 16:32]), F.Copy, after=[du, vu4])
-    v = vec("copy", T.up[:, 0:256], T.ub[:, 0:4].indirect(T.u4[:, 0:16]), after=[du, vu4])
-    vqu = vec("quant", T.cu[:], T.su[:], T.up[:], after=[v, s])
-    vec("tt", T.hc[:], T.ip[:, 0:1], T.i15[:, 0:1], A.subtract, after=[v15])
-    vec("ts", T.fx[:], T.y17[:], 1, 72.0, A.is_equal, A.mult, after=[va])
+    vrz = vec("set", T.rz[:, 0:136:8], 0.0, after=[v1])
+    vec("tt", T.hc[:], T.ip[:, 0:1], T.i15[:, 0:1], A.subtract, after=[va])
+    vec("ts", T.fx[:], T.y17[:], 1, 72.0, A.is_equal, A.mult)
     vec("ts", T.fy[:], T.y17[:], 16, 64.0, A.is_equal, A.mult)
     vec("ts", T.fz[:], T.a14[:], 4.0, 7.0, A.mult, A.add)
     vf = vec("ts", T.fw[:], T.a112[:], 0.5, 7.0, A.mult, A.add)
+    vec("ts", T.fo[:, 0:1], T.fx[:], T.fy[:], T.fz[:], A.add, A.add, after=[vf])
+    vfo = vec("ts", T.fo[:, 1:2], T.fx[:], T.fy[:], T.fw[:], A.add, A.add)
+    vval = vec("ts", T.val[:], T.vb[:], T.hc[:], -256.0, A.add, A.add, after=[pvb])
+    v = vec("quant", T.cq[:], T.sq[:], T.up[:], after=[du])
+    vqu = (vec("copy", T.cu[:].bitcast(dt.uint32), T.cq[:].bitcast(dt.uint32).indirect(T.u0[:]), after=[v]),
+           act(T.su[:], T.sq[:].indirect(T.u0[:]), F.Copy, after=[v]))
 
-    def constants():
-        vec("ts", T.fo[:, 0:1], T.fx[:], T.fy[:], T.fz[:], A.add, A.add, after=[vf])
-        vfo = vec("ts", T.fo[:, 1:2], T.fx[:], T.fy[:], T.fw[:], A.add, A.add)
-        vrz = vec("ts", T.rz[:], T.ri[:], 0, None, A.is_gt, after=[pri])
-        vval = vec("ts", T.val[:], T.vb[:], T.hc[:], -256.0, A.add, A.add, after=[pvb, vf])
-        return vfo, vrz, vval
-
-    def score_half(h, toks, row_first):
-        def row():
-            return mm(T.ps[:, 512 * h:512 * h + H], T.cu[:], T.su[:], T.cx[:, H * h:H * h + H], T.sx[:, H * h:H * h + H])
-
+    def score_half(h, toks):
         wait("t", *toks)
-        r = row() if row_first else None
         for t in (2 * h, 2 * h + 1):
             x = mm(T.ps[:, 512 * (2 + t):512 * (2 + t) + 128], T.cx[:, 128 * t:128 * t + 128],
                    T.sx[:, 128 * t:128 * t + 128], T.cu[:], T.su[:])
-        return x, r or row()
+        r = {b: mm(T.ps[:, 512 * b:512 * b + H], T.cu[:], T.su[:], T.cx[:, H * h:H * h + H], T.sx[:, H * h:H * h + H])
+             for b in ((0, 6), (7, 1))[h]}
+        return x, r[h], r[6 + h]
 
     def column(h, tx):
-        return act(T.sc4[:, 2 * h:2 * h + 2], T.ps[:, 512 * (2 + 2 * h):512 * (4 + 2 * h):512], F.Copy, after=[tx])
+        ps = T.ps[:, 512 * (2 + 2 * h):512 * (4 + 2 * h):512]
+        return (act(T.sc4[:, 2 * h:2 * h + 2], ps, F.Copy, after=[tx]),
+                act(T.nd[:, 2 * h:2 * h + 2], ps, F.Abs, scale=STEP, bias=TINY))
 
     def inside(h, sc):
-        n = act(T.nd[:, 2 * h:2 * h + 2], T.ps[:, 512 * (2 + 2 * h):512 * (4 + 2 * h):512], F.Abs, scale=STEP, bias=TINY)
-        return [act(T.th[:, 128 * t:128 * t + 128], T.dm[:], F.Identity, after=[sc, n, pdm],
+        return [act(T.th[:, 128 * t:128 * t + 128], T.dm[:], F.Identity, after=[*sc, pdm],
                     scale=T.nd[:, t:t + 1], bias=T.sc4[:, t:t + 1]) for t in (2 * h, 2 * h + 1)]
+
+    def signs(t, j0, j1, toks):
+        p = 512 * (6 + j0 // H) + j0 % H
+        return act(T.fl[:, 512 * t + j0:512 * t + j1], T.ps[:, p:p + j1 - j0], F.Sign, scale=-1.0, bias=T.sc4[:, t:t + 1],
+                   after=toks)
+
+    def counted(t, j0, j1, i, tok):
+        fl = T.fl[:, 512 * t + j0:512 * t + j1]
+        how = (F.Relu, -1.0, 0.0) if lower else (F.Sign, 1.0, 1.0)
+        return act(fl, fl, how[0], scale=how[1], bias=how[2], accum_out=T.pl[:, i:i + 1], after=[tok])
 
     def plain(t, j0, j1, at, toks=()):
         p = 512 * (j0 // H) + j0 % H
@@ -144,38 +150,16 @@ def rank_program(g, core, T, topo):
         return vec("tt", T.fl[:, 512 * t + at:512 * t + at + 128], T.ps[:, p:p + 128], T.th[:, 128 * t:128 * t + 128],
                    A.is_gt if lower else A.is_le, after=[tok])
 
-    def total(t, i0, i1, tok):
-        fl = T.fl[:, 512 * t + i0:512 * t + i1]
-        return act(fl, fl, F.Copy, after=[tok], accum_out=T.pl[:, t:t + 1])
-
-    def halves(z, cs, j, tok):
-        return vec("scan", cs[:, j:j + 128], T.fl[:, z:z + 128], T.fl[:, z + 128:z + 256], 0.0, A.add, A.add, after=[tok])
+    def halves(z, j, tok, n=128):
+        return vec("scan", T.cs[:, j:j + n], T.fl[:, z:z + n], T.fl[:, z + n:z + 2 * n], 0.0, A.add, A.add, after=[tok])
 
     def row_sum(t, tok):
-        z, j = 512 * t, 256 * (t // 2)
+        z, j = 512 * t, 256 * (t % 2)
         return vec("scan", T.ce[:, j:j + 256], T.fl[:, z:z + 256], T.fl[:, z + 256:z + 512], -256.0, A.add, A.add, after=[tok])
 
-    def cross(t, h, at, toks=()):
-        return plain(t, H * h, H * h + H, at, toks)
-
-    def places(f, k, sc, trk):
-        a = cross(2 * f, k, H, [trk])
-        b = cross(2 * f + 1, k, H)
-        th = inside(k, sc)
-        s0 = total(2 * f, 0, 512, a)
-        cross(2 * k, f, 0, [sc])
-        row_sum(2 * f + 1, b)
-        plain(2 * k, H * k + 128, H * k + 256, H + 128)
-        s1 = total(2 * k, 0, 512, diag(2 * k, H, th[0]))
-        t = 2 * k + 1
-        cross(t, f, 0)
-        plain(t, H * k, H * k + 128, H)
-        e = row_sum(t, diag(t, H + 128, th[1]))
-        vec("ts", T.pou[:, 1:4:2], T.ce[:, 255:512:256], 256.0, None, A.add, after=[e])
-        return vec("copy", T.pou[:, 0:4:2], T.pl[:, 0:4:2], after=[s0, s1])
-
-    def to_list(e, val, out, w0, w1, n):
+    def to_list(e, val, out, w0, w1, n, beside=lambda: None):
         e = vec("copy", T.win[:, 32:w1].indirect(T.pou[:]), val[:], after=[e, vval, vwin])
+        beside()
         vec("tr", T.wt[:, 0:256], T.win[:, w0:w0 + 256], after=[e])
         e = vec("tr", T.wt[:, 256:544], T.win[:, w0 - 16:w0 + 272])
         runs = [(0, 128, 0, 0), (0, 64, 2, 1), (2, 64, 0, 1), *[(d, 32, d ^ 1, 2) for d in range(4)],
@@ -192,20 +176,34 @@ def rank_program(g, core, T, topo):
         return v, act(s_to[:, j:j + K], s[:].indirect(off[:, 0:16]), F.Copy, after=toks)
 
     vq = vec("quant", T.cx[:, 0:H], T.sx[:, 0:H], T.xb[:, 0:1024], after=[dx[0]])
-    tx, tr0 = score_half(0, [vqu, vq], False)
+    tx, tr0, ts0 = score_half(0, [*vqu, vq])
     sc0 = column(0, tx)
     th0 = inside(0, sc0)
-    vfo, vrz, vval = constants()
+    s2 = counted(0, 128, 256, 2, signs(0, 128, 256, [ts0]))
     vq = vec("quant", T.cx[:, H:2 * H], T.sx[:, H:2 * H], T.xb[:, 1024:2048], after=[dx[1]])
-    plain(0, 128, 256, 128, [sc0, tr0])
-    plain(1, 0, 128, 0)
-    diag(0, 0, th0[0])
-    diag(1, 128, th0[1])
-    tx, tr1 = score_half(1, [vq], True)
-    tall = mm(T.ps[:, 3072:3584], T.cu[:], T.su[:], T.cx[:], T.sx[:])
-    vpl = places(0, 1, column(1, tx), tr1)
-    srows = act(T.rows[:], T.ps[:, 3072:3584], F.Copy, after=[tall])
-    zl, ql = to_list(vpl, T.val, T.lst, w0, 544, 5)
+    tx, tr1, ts1 = score_half(1, [vq])
+    plain(1, 0, 128, 0, [sc0[0], tr0])
+    d = diag(0, 0, th0[0]), diag(1, 128, th0[1])
+    halves(0, 0, d[0], 64)
+    halves(512, 128, d[1])
+    sc1 = column(1, tx)
+    s0 = signs(0, H, 512, [ts1])
+    th1 = inside(1, sc1)
+    s1 = signs(1, H, 512, [])
+    s0, s1 = counted(0, H, 512, 0, s0), counted(1, H, 512, 1, s1)
+    for h in (0, 1):
+        srows = act(T.rows[:, H * h:H * h + H], T.ps[:, 512 * (6 + h):512 * (6 + h) + H], F.Copy)
+    plain(2, 0, H, 0, [sc1[0]])
+    plain(3, 0, H, 0)
+    plain(2, 384, 512, 384, [tr1])
+    plain(3, H, 384, H)
+    d = diag(2, H, th1[0]), diag(3, 384, th1[1])
+    row_sum(2, d[0])
+    e = row_sum(3, d[1])
+    vec("ts", T.pou[:, 0:1], T.cs[:, 63:64], T.pl[:, 0:1], T.pl[:, 2:3], A.add, A.add, after=[s0, s2])
+    vec("ts", T.pou[:, 1:2], T.cs[:, 255:256], T.pl[:, 1:2], None, A.add, after=[s1])
+    vpl = vec("ts", T.pou[:, 2:4], T.ce[:, 255:512:256], 256.0, None, A.add, after=[e])
+    zl, ql = to_list(vpl, T.val, T.lst, w0, 544, 6)
 
     def send(c, s, j, to, arr, out, pk):
         rid, pid, _ = topo.addr(T.cores[to])
@@ -220,21 +218,19 @@ def rank_program(g, core, T, topo):
     def note(dst, src, to, what, *toks):
         rid, pid, _ = topo.addr(T.cores[to])
         wait("g", *toks)
-        g.remote_dma(dst, src, T.sem["a" + what], T.sem["o" + what], pid, rid,
-                     sum(1 << e for e in topo.engines(core, T.cores[to])[0:8]))
-        return ("a" + what, 8), ("o" + what, 8)
+        g.remote_dma(dst, src, T.sem["a" + what], T.sem["o" + what], pid, rid, topo.mask(core, T.cores[to]))
+        n = len(topo.engines(core, T.cores[to]))
+        return ("a" + what, n), ("o" + what, n)
 
     def tell(what, me, *toks):
-        tr, arr = [], {}
-        for r, e0, n in ((mate, 0, 8), (other, 8, 4), (other ^ 1, 12, 4)):
-            rid, pid, _ = topo.addr(T.cores[r])
-            eng = topo.engines(core, T.cores[r])[e0:e0 + n]
-            tr.append(RemoteDMATransfer(dst_ids=[DstId(rid=rid, pnc=pid)], dma_engine_mask=sum(1 << e for e in eng),
-                                        remote_sem=T.sem["a%s%d" % (what, rank)], src=me, dst=T["%s%d" % (what, rank)][:]))
-            arr[r] = ("a%s%d" % (what, r), n)
+        to = (other, other ^ 1, mate)
+        m, n = topo.mask(core, T.cores[other]), len(topo.engines(core, T.cores[other]))
+        ids = [DstId(rid=topo.addr(T.cores[r])[0], pnc=topo.addr(T.cores[r])[1]) for r in to]
+        tr = RemoteDMATransfer(dst_ids=ids, dma_engine_mask=m, remote_sem=T.sem["a%s%d" % (what, rank)], src=me,
+                               dsts=[T["%s%d" % (what, rank)][:]] * 3)
         wait("g", *toks)
-        g.remote_dma_fused(tr, local_sem=T.sem["o" + what])
-        return arr, ("o" + what, 16)
+        g.remote_dma_fused([tr], local_sem=T.sem["o" + what])
+        return {r: ("a%s%d" % (what, r), n) for r in to}, ("o" + what, n)
 
     snum = act(T.nme[:], T.zs[:, 7:64:8], F.Copy, after=[zl])
     arrn, outn = note(T.nth[:], T.nme[:], mate, "n", snum)
@@ -271,7 +267,7 @@ def rank_program(g, core, T, topo):
     c = [vec("ts", T.fl[:, 1024 + H * i:1280 + H * i], T.rv[:], kk(mate)[:, i:i + 1], None, A.is_ge if lower else A.is_gt,
              after=[arrk[mate], srv]) for i in (0, 1)]
     vl = vec("tt", T.lose[:], kme, kk(mate)[:], A.is_lt if lower else A.is_le)
-    c = [halves(1024 + H * i, T.cs, 128 * i, c[i]) for i in (0, 1)]
+    c = [halves(1024 + H * i, 128 * i, c[i]) for i in (0, 1)]
     for i in (0, 1):
         at = 2 * f2 + i
         vmsg = vec("ts", msg[:, at:at + 1], T.cs[:, 128 * i + 127:128 * i + 128], T.kb[:, i:i + 1], T.lose[:, i:i + 1],
@@ -292,37 +288,34 @@ def rank_program(g, core, T, topo):
     vh = vec("tt", T.h4[:], T.h3[:], T.dn[:], A.mult, after=[vh, vdn])
     vc = vec("copy", T.q1[:], T.h2[:], after=[v])
     vpn = vec("tt", T.pme[:, 0:8], T.h4[:], nl[:], A.add, after=[vh])
-    p2 = pick(T.c2, T.s2, H * f2, T.c1, T.s1, T.q1, vc, arr1, *p1)
     spn = act(T.pme[:, 8:9], mine, F.Copy, after=[vm1])
+    p2 = pick(T.c2, T.s2, H * f2, T.c1, T.s1, T.q1, vc, arr1, *p1)
 
-    arr2, out2 = send(T.c2, T.s2, H * f2, other, "a2", "o2", p2)
     arrp, outp = note(T.pth[:, 0:9], T.pme[:, 0:9], other, "p", vpn, spn)
+    arr2, out2 = send(T.c2, T.s2, H * f2, other, "a2", "o2", p2)
 
     def replicated(h, src, *toks):
         return act(T.rep[:, H * h:H * h + H], src[:, 0:8].indirect(T.r32[:]), F.Copy, after=[vr32, *toks])
 
-    def turned(h, tok):
-        return vec("tr", T.colr[:, H * h:H * h + H], T.rep[:, H * h:H * h + H], after=[tok])
-
     def who(h, m, *toks):
         return vec("ts", T.whow[:, H * h:H * h + H], T.iot[:], m, 2.0 * h, A.is_ge, A.add, after=[piot, *toks])
 
-    s = replicated(f2, T.pme, vpn)
+    replicated(f2, T.pme, vpn)
     who(f2, mine)
-    turned(f2, s)
 
-    v = vec("tt", T.t1[:], msg[:], T["m%d" % mate][:], A.add, after=[*smsg, arrm[mate]])
+    v = vec("tt", T.t1[:], msg[:], T["m%d" % other][:], A.add, after=[*smsg, arrm[other]])
     for i in range(4):
-        e = vec("ts", T.pou[:, i:i + 1], T.t1[:, i:i + 1], T["m%d" % other][:, i:i + 1], T["m%d" % (other ^ 1)][:, i:i + 1],
-                A.add, A.add, after=[v, arrm[other], arrm[other ^ 1]])
-    v2 = to_list(e, T.val2, T.q2, 32, 800, 5)[1]
+        e = vec("ts", T.pou[:, i:i + 1], T.t1[:, i:i + 1], T["m%d" % mate][:, i:i + 1], T["m%d" % (other ^ 1)][:, i:i + 1],
+                A.add, A.add, after=[v, arrm[mate], arrm[other ^ 1]])
+    s = replicated(k2, T.pth, arrp)
+    v2 = to_list(e, T.val2, T.q2, 32, 800, 6, lambda: who(k2, T.pth[:, 8:9], arrp))[1]
 
     p3 = pick(T.c3, T.s3, 0, T.c2, T.s2, T.q2, v2, arr2, *p2)
     ty = [mm(T.ps[:, 512 * (4 + o):512 * (4 + o) + K], T.cw[:, 128 * o:128 * o + 128], T.sw[:, 128 * o:128 * o + 128],
              T.c3[:], T.s3[:], after=[vw, *p3]) for o in range(O)]
-    s = replicated(k2, T.pth, arrp)
-    vw2 = who(k2, T.pth[:, 8:9], arrp)
-    ids = [vec("copy", T.idf[:, 0:32], T.whow[:].indirect(T.q2[:, 16:18]), after=[vw2])]
+    v = vec("tr", T.colr[:], T.rep[:], after=[s])
+    ids = [act(T.idf[:, 0:32], T.whow[:].indirect(T.q2[:, 16:18]), F.Copy),
+           vec("ts", T.idf[:, 32:64], T.colr[:].indirect(T.q2[:, 16:18]), 256.0, None, A.add, after=[v])]
 
     def store(y, out, in_, tok):
         wait(y, tok)
@@ -330,20 +323,15 @@ def rank_program(g, core, T, topo):
 
     def result(o):
         ab = T.ysb[:, K * o:K * o + K], T.ps[:, 512 * (4 + o):512 * (4 + o) + K]
-        return vec("copy", *ab, after=[ty[o]]) if o % 2 == 0 else act(*ab, F.Copy, after=[ty[o]])
+        return vec("copy", *ab, after=[ty[o]]) if o in (1, 2) else act(*ab, F.Copy, after=[ty[o]])
 
     def store_y(y, o, tok):
         store(y, T.y[:, K * o:K * o + K], T.ysb[:, K * o:K * o + K], tok)
 
-    store("y", T.id[0:1, :], T.idf[0:128:16, 0:32], ids[0])
-    store_y("y", 0, result(0))
-    v = turned(k2, s)
-    store_y("y", 1, result(1))
-    r2 = result(2)
-    ids.append(vec("ts", T.idf[:, 32:64], T.colr[:].indirect(T.q2[:, 16:18]), 256.0, None, A.add, after=[v]))
-    store_y("s", 3, result(3))
-    store_y("y", 2, r2)
-    store("s", T.id[1:2, :], T.idf[0:128:16, 32:64], ids[1])
+    for i in (0, 1):
+        store("y", T.id[i:i + 1, :], T.idf[0:128:16, 32 * i:32 * i + 32], ids[i])
+    for o in range(O):
+        store_y("y" if o < 3 else "s", o, result(o))
 
     wait("g", out1, outn, outk, out2, outm, outp, arr1, arr2, arrn, arrp, *arrk.values(), *arrm.values(),
          *[(s, n) for s, n in cnt.items()])

@@ -14,15 +14,15 @@ def _bufs(dtype, **widths):
 _bufs("float8_e4m3fn_x4", cx=512, cq=128, cu=128, cw=512, c1=512, c2=512, c3=256)
 _bufs("uint8", sx=512, sq=128, su=128, sw=512, s1=512, s2=512, s3=256)
 _bufs("bfloat16", xb=2048, wb=2048, up=512, neg=128, dm=128, fl=2048, cs=256, ce=512, f1=256, g1=128,
-      val=64, val2=64, win=800, wt=544, z=136, zs=136, rz=136, iot=256, rep=512, colr=512, whow=512,
+      val=64, val2=64, win=800, wt=544, z=136, zs=136, rz=136, iot=256, rep=512, tab=512,
       nme=8, nth=8, pme=16, pth=16)
-_bufs("float32", sc4=4, nd=4, th=512, pl=4, vb=64, vb2=64, hc=1, hc2=1, fx=1, fy=1, fz=1, fw=1, k16=16, k256=16, kb=2,
+_bufs("float32", sc4=4, nd=4, th=512, pl=4, vb=64, vb2=64, hc=1, fx=1, fy=1, fz=1, fw=1, k16=16, k256=16, kb=2,
       k32=8, rv=256, rows=512, sg=32, sgt=32, h1=16, h2=16, dn=8, h3=8, h4=8, k0=2, k1=2, k2=2, k3=2, m0=4, m1=4, m2=4,
-      m3=4, lose=2, cp=2, t1=4, idf=64, ysb=1024)
-_bufs("int32", ip=16, i15=16, c16=16, c2i=16, y17=1, a14=1, a112=1, a96=8, kb0=2, k320=8)
-_bufs("uint16", u0=8, pou=4, fo=2, r32=16, lst=32, q1=16, q2=32)
-SEMAPHORES = ["cv", "ca", "ct", "cp", "du", "dx0", "dx1", "dw", "dy0", "dy1", "a1", "o1", "a2", "o2", "on", "ok", "om", "op",
-              "an", "ap", "ak0", "ak1", "ak2", "ak3", "am0", "am1", "am2", "am3"]
+      m3=4, lose=2, cp=2, t1=4, idf=64, yy=2048, ysb=1024, fv=1, up256=1)
+_bufs("int32", ip=16, i15=16, c16=16, y17=1, a14=1, a112=1, a48=1, a2=1)
+_bufs("uint16", u0=8, pou=4, fo=4, lst=32, q1=16, q2=32)
+SEMAPHORES = ["cv", "ca", "ct", "cp", "du", "dx0", "dx1", "dw", "dy0", "dy1", "a1", "o1", "on", "ok", "om", "op",
+              "a2", "o2", "an", "ap", "ak0", "ak1", "ak2", "ak3", "am0", "am1", "am2", "am3"]
 STEP, TINY = 1.125 * 2.0 ** -24, 2.0 ** -124
 
 
@@ -82,11 +82,18 @@ def rank_program(g, core, T, topo):
     wait("g", vneg)
     pdm = inc("cp", g.affine_select(T.dm[:], T.neg[:], [[-1, 128]], A.is_gt if lower else A.is_ge, 0.0, 0, 1))
     pc16 = inc("cp", g.iota(T.c16[:], [[16, 16]], 0, 0))
-    pc2 = inc("cp", g.iota(T.c2i[:], [[1, 8], [0, 2]], 0, 0))
     piot = inc("cp", g.iota(T.iot[:], [[1, 256]], -256, 0, **f))
-    inc("cp", g.iota(T.kb0[:], [[-32 if lower else 32, 2]], 255 if lower else 0, -1 if lower else 1))
-    inc("cp", g.iota(T.k320[:], [[32, 8]], -256, 1))
-    pvb2 = inc("cp", g.iota(T.vb2[:], [[256, 2], [32, 2], [1, 16]], -256, 0, **f))
+    sg = -1 if lower else 1
+    wait("g", piot)
+    for r in range(4):
+        run = slice(32 * r, 32 * r + 32)
+        inc("cp", g.iota(T.kb[run, :], [[32 * sg, 2]], 64 * r * sg + (255 if lower else 0), sg, **f))
+        inc("cp", g.iota(T.k32[run, :], [[32, 8]], -256, 1, **f))
+        p = inc("cp", g.iota(T.vb2[run, :], [[256, 2], [32, 2], [1, 16]], 32 * r - 256, 0, **f))
+    wait("g", p)
+    inc("cp", g.iota(T.up256[0:64, :], [[0, 1]], 0, 0, **f))
+    inc("cp", g.iota(T.up256[64:128, :], [[0, 1]], 256, 0, **f))
+    pvb2 = inc("cp", g.iota(T.rep[64:128, :], [[0, 512]], 0, 0, **f))
     w0 = 32 if lower else 32 + H
     vec("set", T.up[:, 8:512], 0.0)
     vec("set", T.u0[:], 0)
@@ -101,10 +108,7 @@ def rank_program(g, core, T, topo):
     vec("ts", T.fy[:], T.y17[:], 16, 64.0, A.is_equal, A.mult)
     vec("ts", T.fz[:], T.a14[:], 4.0, 7.0, A.mult, A.add)
     vf = vec("ts", T.fw[:], T.a112[:], 0.5, 7.0, A.mult, A.add)
-    vec("ts", T.fo[:, 0:1], T.fx[:], T.fy[:], T.fz[:], A.add, A.add, after=[vf])
-    vfo = vec("ts", T.fo[:, 1:2], T.fx[:], T.fy[:], T.fw[:], A.add, A.add)
-    vval = vec("ts", T.val[:], T.vb[:], T.hc[:], -256.0, A.add, A.add, after=[pvb])
-    v = vec("quant", T.cq[:], T.sq[:], T.up[:], after=[du])
+    v = vec("quant", T.cq[:], T.sq[:], T.up[:], after=[du, v1])
     vqu = (vec("copy", T.cu[:].bitcast(dt.uint32), T.cq[:].bitcast(dt.uint32).indirect(T.u0[:]), after=[v]),
            act(T.su[:], T.sq[:].indirect(T.u0[:]), F.Copy, after=[v]))
 
@@ -157,8 +161,8 @@ def rank_program(g, core, T, topo):
         z, j = 512 * t, 256 * (t % 2)
         return vec("scan", T.ce[:, j:j + 256], T.fl[:, z:z + 256], T.fl[:, z + 256:z + 512], -256.0, A.add, A.add, after=[tok])
 
-    def to_list(e, val, out, w0, w1, n, beside=lambda: None):
-        e = vec("copy", T.win[:, 32:w1].indirect(T.pou[:]), val[:], after=[e, vval, vwin])
+    def to_list(toks, val, out, w0, w1, fo, beside=lambda: None, beside2=lambda: None):
+        e = vec("copy", T.win[:, 32:w1].indirect(T.pou[:]), val[:], after=[*toks, vval, vwin])
         beside()
         vec("tr", T.wt[:, 0:256], T.win[:, w0:w0 + 256], after=[e])
         e = vec("tr", T.wt[:, 256:544], T.win[:, w0 - 16:w0 + 272])
@@ -167,19 +171,25 @@ def rank_program(g, core, T, topo):
         toks = []
         for i, (d, m, src, j) in enumerate(runs):
             ab = T.z[32 * d:32 * d + m, j:136:4], T.wt[32 * src:32 * src + m, 0:544:16]
-            toks.append(vec("copy", *ab, after=[e]) if i < 11 - n else act(*ab, F.Copy, after=[e]))
+            toks.append(vec("copy", *ab, after=[e]) if i < 5 else act(*ab, F.Copy, after=[e]))
+        beside2()
         e = vec("scan", T.zs[:], T.rz[:], T.z[:], 0.0, A.mult, A.add, after=[*toks, vrz])
-        return e, vec("ts", out[:], T.zs[:].indirect(T.fo[:, 0:2]), 256.0, None, A.add, after=[e, vfo])
+        return e, vec("ts", out[:], T.zs[:].indirect(T.fo[:, fo:fo + 2]), 256.0, None, A.add, after=[e, vfo])
 
-    def pick(c_to, s_to, j, c, s, off, *toks):
-        v = vec("copy", c_to[:, j:j + K].bitcast(dt.uint32), c[:].bitcast(dt.uint32).indirect(off[:, 0:16]), after=toks)
-        return v, act(s_to[:, j:j + K], s[:].indirect(off[:, 0:16]), F.Copy, after=toks)
+    def pick(c_to, s_to, j, c, s, off, *toks, n=K):
+        v = vec("copy", c_to[:, j:j + n].bitcast(dt.uint32), c[:].bitcast(dt.uint32).indirect(off), after=toks)
+        return v, act(s_to[:, j:j + n], s[:].indirect(off), F.Copy, after=toks)
 
     vq = vec("quant", T.cx[:, 0:H], T.sx[:, 0:H], T.xb[:, 0:1024], after=[dx[0]])
     tx, tr0, ts0 = score_half(0, [*vqu, vq])
+    for out, bits in ((T.a48, 48), (T.a2, 2)):
+        vec("ts", out[:], T.ip[:, 0:1], bits, None, A.bitwise_and)
+    vec("ts", T.fo[:, 0:1], T.fx[:], T.fy[:], T.fz[:], A.add, A.add, after=[vf])
+    vfo = vec("ts", T.fo[:, 1:2], T.fx[:], T.fy[:], T.fw[:], A.add, A.add)
+    vval = vec("ts", T.val[:], T.vb[:], T.hc[:], -256.0, A.add, A.add, after=[pvb])
     sc0 = column(0, tx)
     th0 = inside(0, sc0)
-    s2 = counted(0, 128, 256, 2, signs(0, 128, 256, [ts0]))
+    s2 = signs(0, 128, 256, [ts0])
     vq = vec("quant", T.cx[:, H:2 * H], T.sx[:, H:2 * H], T.xb[:, 1024:2048], after=[dx[1]])
     tx, tr1, ts1 = score_half(1, [vq])
     plain(1, 0, 128, 0, [sc0[0], tr0])
@@ -187,6 +197,7 @@ def rank_program(g, core, T, topo):
     halves(0, 0, d[0], 64)
     halves(512, 128, d[1])
     sc1 = column(1, tx)
+    s2 = counted(0, 128, 256, 2, s2)
     s0 = signs(0, H, 512, [ts1])
     th1 = inside(1, sc1)
     s1 = signs(1, H, 512, [])
@@ -201,9 +212,9 @@ def rank_program(g, core, T, topo):
     row_sum(2, d[0])
     e = row_sum(3, d[1])
     vec("ts", T.pou[:, 0:1], T.cs[:, 63:64], T.pl[:, 0:1], T.pl[:, 2:3], A.add, A.add, after=[s0, s2])
-    vec("ts", T.pou[:, 1:2], T.cs[:, 255:256], T.pl[:, 1:2], None, A.add, after=[s1])
+    v = vec("ts", T.pou[:, 1:2], T.cs[:, 255:256], T.pl[:, 1:2], None, A.add, after=[s1])
     vpl = vec("ts", T.pou[:, 2:4], T.ce[:, 255:512:256], 256.0, None, A.add, after=[e])
-    zl, ql = to_list(vpl, T.val, T.lst, w0, 544, 6)
+    zl, ql = to_list((v, vpl), T.val, T.lst, w0, 544, 0)
 
     def send(c, s, j, to, arr, out, pk):
         rid, pid, _ = topo.addr(T.cores[to])
@@ -234,24 +245,24 @@ def rank_program(g, core, T, topo):
 
     snum = act(T.nme[:], T.zs[:, 7:64:8], F.Copy, after=[zl])
     arrn, outn = note(T.nth[:], T.nme[:], mate, "n", snum)
-    v = vec("copy", T.sg[:], T.rows[:].indirect(T.lst[:, 16:18]), after=[ql, srows])
-    vk = vec("tr", T.sgt[:], T.sg[:], after=[v])
+    s = act(T.sg[:], T.rows[:].indirect(T.lst[:, 16:18]), F.Copy, after=[ql, srows])
+    pick(T.c1, T.s1, a0, T.cx, T.sx, T.lst[:, 0:8], ql, n=128)
+    vk = vec("tr", T.sgt[:], T.sg[:], after=[s])
     kme = T.sgt[:, 15:17]
     arrk, outk = tell("k", kme, vk)
 
-    p1 = pick(T.c1, T.s1, a0, T.cx, T.sx, T.lst, ql)
+    p1 = pick(T.c1, T.s1, a0 + 128, T.cx, T.sx, T.lst[:, 8:16], ql, n=128)
     arr1, out1 = send(T.c1, T.s1, a0, mate, "a1", "o1", p1)
 
     t = mm(T.ps[:, 0:256], T.cu[:], T.su[:], T.c1[:, a0:a0 + H], T.s1[:, a0:a0 + H], after=p1)
     srv = act(T.rv[:], T.ps[:, 0:256], F.Copy, after=[t])
-    v = vec("ts", T.a96[:], T.ip[:, 0:8], 96, None, A.bitwise_and)
-    vr32 = vec("copy", T.r32[:], T.c2i[:], after=[pc2])
+    vec("ts", T.fo[:, 2:3], T.fx[:], T.fy[:], T.fz[:], A.add, A.add)
+    vec("ts", T.fw[:], T.a2[:], 4.0, 7.0, A.mult, A.add)
+    vfv = vec("tt", T.fv[:], T.a48[:], T.fx[:], A.add)
     vk16 = vec("tt", T.k16[:], T.i15[:], T.c16[:], A.add, after=[pc16])
-    vec("tt", T.kb[:], T.kb0[:], T.a96[:, 0:2], A.subtract if lower else A.add, after=[v, pvb2])
-    vec("tt", T.k32[:], T.k320[:], T.a96[:], A.subtract)
-    v = vec("tt", T.hc2[:], T.a112[:], T.a96[:, 0:1], A.add)
+    vec("ts", T.val2[:], T.vb2[:], T.hc[:], None, A.add, after=[pvb2])
     vec("ts", T.k256[:], T.k16[:], -256.0, None, A.add, after=[vk16])
-    vec("ts", T.val2[:], T.vb2[:], T.hc2[:], None, A.add, after=[v])
+    vec("ts", T.fo[:, 3:4], T.fv[:], T.fy[:], T.fw[:], A.add, A.add, after=[vfv])
     vw = vec("quant", T.cw[:], T.sw[:], T.wb[:], after=[dw])
     vwin = vec("set", T.win[:, 16:304], 0.0)
 
@@ -268,16 +279,16 @@ def rank_program(g, core, T, topo):
              after=[arrk[mate], srv]) for i in (0, 1)]
     vl = vec("tt", T.lose[:], kme, kk(mate)[:], A.is_lt if lower else A.is_le)
     c = [halves(1024 + H * i, 128 * i, c[i]) for i in (0, 1)]
+    row = mm(T.ps[:, 512:768], T.cu[:], T.su[:], T.c1[:, b0:b0 + H], T.s1[:, b0:b0 + H], after=[arr1])
+    theirs = T.ps[:, 512:768]
+    rows = (T.rv[:], theirs) if lower else (theirs, T.rv[:])
+    v = vec("tt", T.f1[:], rows[0], rows[1], A.is_ge, after=[row])
     for i in (0, 1):
         at = 2 * f2 + i
         vmsg = vec("ts", msg[:, at:at + 1], T.cs[:, 128 * i + 127:128 * i + 128], T.kb[:, i:i + 1], T.lose[:, i:i + 1],
                    A.add, A.mult, after=[c[i], vl])
     arrm, outm = tell("m", msg[:], vmsg, *smsg)
 
-    row = mm(T.ps[:, 512:768], T.cu[:], T.su[:], T.c1[:, b0:b0 + H], T.s1[:, b0:b0 + H], after=[arr1])
-    theirs = T.ps[:, 512:768]
-    rows = (T.rv[:], theirs) if lower else (theirs, T.rv[:])
-    v = vec("tt", T.f1[:], rows[0], rows[1], A.is_ge, after=[row])
     mine = T.g1[:, 127:128]
     vm1 = vec("scan", T.g1[:], T.f1[:, 0:128], T.f1[:, 128:256], -256.0, A.add, A.add, after=[v])
     nl, nu = (T.nme, T.nth) if lower else (T.nth, T.nme)
@@ -289,49 +300,59 @@ def rank_program(g, core, T, topo):
     vc = vec("copy", T.q1[:], T.h2[:], after=[v])
     vpn = vec("tt", T.pme[:, 0:8], T.h4[:], nl[:], A.add, after=[vh])
     spn = act(T.pme[:, 8:9], mine, F.Copy, after=[vm1])
-    p2 = pick(T.c2, T.s2, H * f2, T.c1, T.s1, T.q1, vc, arr1, *p1)
+    p2 = pick(T.c2, T.s2, H * f2, T.c1, T.s1, T.q1[:], vc, arr1, *p1)
 
     arrp, outp = note(T.pth[:, 0:9], T.pme[:, 0:9], other, "p", vpn, spn)
     arr2, out2 = send(T.c2, T.s2, H * f2, other, "a2", "o2", p2)
 
     def replicated(h, src, *toks):
-        return act(T.rep[:, H * h:H * h + H], src[:, 0:8].indirect(T.r32[:]), F.Copy, after=[vr32, *toks])
+        for j in (0, 16):
+            s = act(T.rep[64:128, H * h + j:H * h + H:32], src[64:128, 0:8], F.Copy, after=toks)
+        return s
 
     def who(h, m, *toks):
-        return vec("ts", T.whow[:, H * h:H * h + H], T.iot[:], m, 2.0 * h, A.is_ge, A.add, after=[piot, *toks])
+        return vec("ts", T.tab[0:64, H * h:H * h + H], T.iot[0:64, :], m[0:64, 8:9], 2.0 * h, A.is_ge, A.add,
+                   after=[piot, *toks])
 
-    replicated(f2, T.pme, vpn)
-    who(f2, mine)
+    def turned(h, tok):
+        return vec("tr", T.tab[64:128, H * h:H * h + H], T.rep[64:128, H * h:H * h + H], after=[tok])
+
+    def products(j, n, b, *toks):
+        ty = [mm(T.ps[:, 512 * (b + o):512 * (b + o) + n], T.cw[:, 128 * o:128 * o + 128], T.sw[:, 128 * o:128 * o + 128],
+                 T.c2[:, j:j + n], T.s2[:, j:j + n], after=toks) for o in range(O)]
+        return [(T.yy[:, 512 * o + j:512 * o + j + n], T.ps[:, 512 * (b + o):512 * (b + o) + n], ty[o]) for o in range(O)]
+
+    def result(out, ps, tok):
+        return act(out, ps, F.Copy, after=[tok])
+
+    sme = replicated(f2, T.pme, vpn)
+    who(f2, T.pme, spn)
+    turned(f2, sme)
+    here = [result(*r) for r in products(H * f2, H, 4, vw, *p2)]
 
     v = vec("tt", T.t1[:], msg[:], T["m%d" % other][:], A.add, after=[*smsg, arrm[other]])
-    for i in range(4):
-        e = vec("ts", T.pou[:, i:i + 1], T.t1[:, i:i + 1], T["m%d" % mate][:, i:i + 1], T["m%d" % (other ^ 1)][:, i:i + 1],
-                A.add, A.add, after=[v, arrm[mate], arrm[other ^ 1]])
+    e = [vec("ts", T.pou[:, i:i + 1], T.t1[:, i:i + 1], T["m%d" % mate][:, i:i + 1], T["m%d" % (other ^ 1)][:, i:i + 1],
+             A.add, A.add, after=[v, arrm[mate], arrm[other ^ 1]]) for i in range(4)]
     s = replicated(k2, T.pth, arrp)
-    v2 = to_list(e, T.val2, T.q2, 32, 800, 6, lambda: who(k2, T.pth[:, 8:9], arrp))[1]
+    ty = products(H * k2, H, 0, arr2)
+    v2 = to_list(e[1::2], T.val2, T.q2, 32, 800, 2, lambda: who(k2, T.pth, arrp), lambda: turned(k2, s))[1]
+    there = [result(*r) for r in ty]
 
-    p3 = pick(T.c3, T.s3, 0, T.c2, T.s2, T.q2, v2, arr2, *p2)
-    ty = [mm(T.ps[:, 512 * (4 + o):512 * (4 + o) + K], T.cw[:, 128 * o:128 * o + 128], T.sw[:, 128 * o:128 * o + 128],
-             T.c3[:], T.s3[:], after=[vw, *p3]) for o in range(O)]
-    v = vec("tr", T.colr[:], T.rep[:], after=[s])
-    ids = [act(T.idf[:, 0:32], T.whow[:].indirect(T.q2[:, 16:18]), F.Copy),
-           vec("ts", T.idf[:, 32:64], T.colr[:].indirect(T.q2[:, 16:18]), 256.0, None, A.add, after=[v])]
-
-    def store(y, out, in_, tok):
-        wait(y, tok)
+    def store(y, out, in_, *toks):
+        wait(y, *toks)
         inc("dy%d" % (y == "s"), q[y].dma_start(out, in_), 16)
 
-    def result(o):
-        ab = T.ysb[:, K * o:K * o + K], T.ps[:, 512 * (4 + o):512 * (4 + o) + K]
-        return vec("copy", *ab, after=[ty[o]]) if o in (1, 2) else act(*ab, F.Copy, after=[ty[o]])
+    def winners(o, j0, j1, on_vector):
+        ab = T.ysb[:, K * o + 16 * j0:K * o + 16 * j1], T.yy[:, 512 * o:512 * o + 512].indirect(T.q2[:, j0:j1])
+        toks = [v2, here[o], there[o]]
+        return vec("copy", *ab, after=toks) if on_vector else act(*ab, F.Copy, after=toks)
 
-    def store_y(y, o, tok):
-        store(y, T.y[:, K * o:K * o + K], T.ysb[:, K * o:K * o + K], tok)
-
-    for i in (0, 1):
-        store("y", T.id[i:i + 1, :], T.idf[0:128:16, 32 * i:32 * i + 32], ids[i])
+    v = vec("ts", T.idf[:], T.tab[:].indirect(T.q2[:, 16:20]), T.up256[:], None, A.add, after=[v2])
+    store("y", T.id[:], T.idf[0:128:16, :], v)
+    done = [[winners(0, 0, 16, True)], [winners(1, 0, 16, True)], [winners(2, 0, 12, True), winners(2, 12, 16, False)],
+            [winners(3, 0, 16, False)]]
     for o in range(O):
-        store_y("y" if o < 3 else "s", o, result(o))
+        store("yyys"[o], T.y[:, K * o:K * o + K], T.ysb[:, K * o:K * o + K], *done[o])
 
     wait("g", out1, outn, outk, out2, outm, outp, arr1, arr2, arrn, arrp, *arrk.values(), *arrm.values(),
          *[(s, n) for s, n in cnt.items()])

@@ -14,14 +14,14 @@ def _bufs(dtype, **widths):
 _bufs("float8_e4m3fn_x4", cx=512, cq=128, cu=128, cw=512, c1=512, c2=512, c3=256)
 _bufs("uint8", sx=512, sq=128, su=128, sw=512, s1=512, s2=512, s3=256)
 _bufs("bfloat16", xb=2048, wb=2048, up=512, neg=128, dm=128, fl=2048, cs=256, ce=512, f1=256, g1=128,
-      val=64, val2=64, win=800, wt=544, z=136, zs=136, rz=136, iot=256, rep=512, tab=512,
-      nme=8, nth=8, pme=16, pth=16)
+      val=64, val2=64, win=800, wt=544, zs=136, rz=136, iot=256, rep=512, tab=512,
+      nme=8, nin=8, nab=8, nth=8, pme=16, pth=16)
 _bufs("float32", sc4=4, nd=4, th=512, pl=4, vb=64, vb2=64, hc=1, fx=1, fy=1, fz=1, fw=1, k16=16, k256=16, kb=2,
       k32=8, rv=256, rows=512, sg=32, sgt=32, h1=16, h2=16, dn=8, h3=8, h4=8, k0=2, k1=2, k2=2, k3=2, m0=4, m1=4, m2=4,
-      m3=4, lose=2, cp=2, t1=4, idf=64, yy=2048, ysb=1024, fv=1, up256=1)
+      m3=4, lose=2, cp=2, t1=4, idf=64, yy=2048, ysb=1024, fu=1, fv=1, up256=1)
 _bufs("int32", ip=16, i15=16, c16=16, y17=1, a14=1, a112=1, a48=1, a2=1)
 _bufs("uint16", u0=8, pou=4, fo=4, lst=32, q1=16, q2=32)
-SEMAPHORES = ["cv", "ca", "ct", "cp", "du", "dx0", "dx1", "dw", "dy0", "dy1", "a1", "o1", "on", "ok", "om", "op",
+SEMAPHORES = ["cv", "ca", "ct", "cp", "du", "dx0", "dx1", "dx2", "dx3", "dw", "dy0", "dy1", "a1", "o1", "on", "ok", "om", "op",
               "a2", "o2", "an", "ap", "ak0", "ak1", "ak2", "ak3", "am0", "am1", "am2", "am3"]
 STEP, TINY = 1.125 * 2.0 ** -24, 2.0 ** -124
 
@@ -71,8 +71,8 @@ def rank_program(g, core, T, topo):
     k2 = 1 - f2
 
     du = inc("du", g.scalar.dma_start(T.up[:, 0:8], T.u[:, 0:8]), 16)
-    dx = [inc("dx%d" % h, g.sync.dma_start(T.xb[:, 1024 * h:1024 * h + 1024], T.x[:, 1024 * h:1024 * h + 1024]), 16)
-          for h in (0, 1)]
+    dx = [inc("dx%d" % t, g.sync.dma_start(T.xb[:, 512 * t:512 * t + 512], T.x[:, 512 * t:512 * t + 512]), 16)
+          for t in range(4)]
     dw = inc("dw", g.sync.dma_start(T.wb[:], T.w[:]), 16)
 
     vneg = vec("set", T.neg[:], -1.0)
@@ -97,62 +97,64 @@ def rank_program(g, core, T, topo):
     w0 = 32 if lower else 32 + H
     vec("set", T.up[:, 8:512], 0.0)
     vec("set", T.u0[:], 0)
+    vec("set", T.pme[0:64, :], 0.0)
     v1 = vec("set", T.rz[:], 1.0)
     vwin = vec("set", T.win[:, w0 - 16:w0 + 272], 0.0)
     v15 = vec("ts", T.i15[:], T.ip[:], 15, None, A.bitwise_and, after=[pip])
-    for out, bits in ((T.y17, 17), (T.a14, 14), (T.a112, 112)):
+    for out, bits in ((T.y17, 17), (T.a14, 14), (T.a112, 112), (T.a48, 48), (T.a2, 2)):
         va = vec("ts", out[:], T.ip[:, 0:1], bits, None, A.bitwise_and)
     vrz = vec("set", T.rz[:, 0:136:8], 0.0, after=[v1])
     vec("tt", T.hc[:], T.ip[:, 0:1], T.i15[:, 0:1], A.subtract, after=[va])
-    vec("ts", T.fx[:], T.y17[:], 1, 72.0, A.is_equal, A.mult)
+    v = vec("ts", T.fx[:], T.y17[:], 1, 72.0, A.is_equal, A.mult)
     vec("ts", T.fy[:], T.y17[:], 16, 64.0, A.is_equal, A.mult)
     vec("ts", T.fz[:], T.a14[:], 4.0, 7.0, A.mult, A.add)
-    vf = vec("ts", T.fw[:], T.a112[:], 0.5, 7.0, A.mult, A.add)
-    v = vec("quant", T.cq[:], T.sq[:], T.up[:], after=[du, v1])
-    vqu = (vec("copy", T.cu[:].bitcast(dt.uint32), T.cq[:].bitcast(dt.uint32).indirect(T.u0[:]), after=[v]),
-           act(T.su[:], T.sq[:].indirect(T.u0[:]), F.Copy, after=[v]))
+    vec("ts", T.fw[:], T.a112[:], 0.5, 7.0, A.mult, A.add)
+    vec("ts", T.fu[:], T.a2[:], 4.0, 7.0, A.mult, A.add)
+    vec("tt", T.fv[:], T.a48[:], T.fx[:], A.add, after=[v])
+    vf = vec("tt", T.k16[:], T.i15[:], T.c16[:], A.add, after=[pc16])
+    vu = vec("quant", T.cq[:], T.sq[:], T.up[:], after=[du, v1])
 
-    def score_half(h, toks):
-        wait("t", *toks)
-        for t in (2 * h, 2 * h + 1):
-            x = mm(T.ps[:, 512 * (2 + t):512 * (2 + t) + 128], T.cx[:, 128 * t:128 * t + 128],
-                   T.sx[:, 128 * t:128 * t + 128], T.cu[:], T.su[:])
-        r = {b: mm(T.ps[:, 512 * b:512 * b + H], T.cu[:], T.su[:], T.cx[:, H * h:H * h + H], T.sx[:, H * h:H * h + H])
-             for b in ((0, 6), (7, 1))[h]}
-        return x, r[h], r[6 + h]
+    def quantised(t):
+        return vec("quant", T.cx[:, 128 * t:128 * t + 128], T.sx[:, 128 * t:128 * t + 128], T.xb[:, 512 * t:512 * t + 512],
+                   after=[dx[t]])
 
-    def column(h, tx):
-        ps = T.ps[:, 512 * (2 + 2 * h):512 * (4 + 2 * h):512]
-        return (act(T.sc4[:, 2 * h:2 * h + 2], ps, F.Copy, after=[tx]),
-                act(T.nd[:, 2 * h:2 * h + 2], ps, F.Abs, scale=STEP, bias=TINY))
+    def down(t, *toks):
+        b = 512 * (2 + t % 2)
+        return mm(T.ps[:, b:b + 128], T.cx[:, 128 * t:128 * t + 128], T.sx[:, 128 * t:128 * t + 128], T.cq[:], T.sq[:], after=toks)
 
-    def inside(h, sc):
-        return [act(T.th[:, 128 * t:128 * t + 128], T.dm[:], F.Identity, after=[*sc, pdm],
-                    scale=T.nd[:, t:t + 1], bias=T.sc4[:, t:t + 1]) for t in (2 * h, 2 * h + 1)]
+    def along(p, j0, j1, *toks):
+        return mm(T.ps[:, p:p + j1 - j0], T.cu[:], T.su[:], T.cx[:, j0:j1], T.sx[:, j0:j1], after=toks)
 
-    def signs(t, j0, j1, toks):
-        p = 512 * (6 + j0 // H) + j0 % H
-        return act(T.fl[:, 512 * t + j0:512 * t + j1], T.ps[:, p:p + j1 - j0], F.Sign, scale=-1.0, bias=T.sc4[:, t:t + 1],
-                   after=toks)
+    ROW_V, ROW_S = (0, 128, 512, 2048), (None, 2560, 3072, 3584)
+
+    def column(t, tx):
+        ps = T.ps[:, 512 * (2 + t % 2):512 * (2 + t % 2) + 1]
+        return (act(T.sc4[:, t:t + 1], ps, F.Copy, after=[tx]), act(T.nd[:, t:t + 1], ps, F.Abs, scale=STEP, bias=TINY))
+
+    def inside(t, sc):
+        return act(T.th[:, 128 * t:128 * t + 128], T.dm[:], F.Identity, after=[*sc, pdm], scale=T.nd[:, t:t + 1],
+                   bias=T.sc4[:, t:t + 1])
+
+    def signs(t, b, *toks):
+        return act(T.fl[:, 512 * t + 128 * b:512 * t + 128 * b + 128], T.ps[:, ROW_S[b]:ROW_S[b] + 128], F.Sign, scale=-1.0,
+                   bias=T.sc4[:, t:t + 1], after=toks)
 
     def counted(t, j0, j1, i, tok):
         fl = T.fl[:, 512 * t + j0:512 * t + j1]
         how = (F.Relu, -1.0, 0.0) if lower else (F.Sign, 1.0, 1.0)
         return act(fl, fl, how[0], scale=how[1], bias=how[2], accum_out=T.pl[:, i:i + 1], after=[tok])
 
-    def plain(t, j0, j1, at, toks=()):
-        p = 512 * (j0 // H) + j0 % H
+    def plain(t, j0, j1, *toks):
+        p = ROW_V[j0 // 128]
         if j1 <= 128 * t:
             op = A.is_ge if lower else A.is_lt
         else:
             op = A.is_gt if lower else A.is_le
-        return vec("ts", T.fl[:, 512 * t + at:512 * t + at + j1 - j0], T.ps[:, p:p + j1 - j0], T.sc4[:, t:t + 1], None,
-                   op, after=toks)
+        return vec("ts", T.fl[:, 512 * t + j0:512 * t + j1], T.ps[:, p:p + j1 - j0], T.sc4[:, t:t + 1], None, op, after=toks)
 
-    def diag(t, at, tok):
-        p = 512 * (t // 2) + 128 * (t % 2)
-        return vec("tt", T.fl[:, 512 * t + at:512 * t + at + 128], T.ps[:, p:p + 128], T.th[:, 128 * t:128 * t + 128],
-                   A.is_gt if lower else A.is_le, after=[tok])
+    def diag(t, *toks):
+        return vec("tt", T.fl[:, 640 * t:640 * t + 128], T.ps[:, ROW_V[t]:ROW_V[t] + 128], T.th[:, 128 * t:128 * t + 128],
+                   A.is_gt if lower else A.is_le, after=toks)
 
     def halves(z, j, tok, n=128):
         return vec("scan", T.cs[:, j:j + n], T.fl[:, z:z + n], T.fl[:, z + n:z + 2 * n], 0.0, A.add, A.add, after=[tok])
@@ -161,60 +163,85 @@ def rank_program(g, core, T, topo):
         z, j = 512 * t, 256 * (t % 2)
         return vec("scan", T.ce[:, j:j + 256], T.fl[:, z:z + 256], T.fl[:, z + 256:z + 512], -256.0, A.add, A.add, after=[tok])
 
-    def to_list(toks, val, out, w0, w1, fo, beside=lambda: None, beside2=lambda: None):
+    def to_list(toks, val, out, w0, w1, fo, beside):
         e = vec("copy", T.win[:, 32:w1].indirect(T.pou[:]), val[:], after=[*toks, vval, vwin])
-        beside()
-        vec("tr", T.wt[:, 0:256], T.win[:, w0:w0 + 256], after=[e])
+        beside[0]()
+        v = vec("tr", T.wt[:, 0:256], T.win[:, w0:w0 + 256], after=[e])
         e = vec("tr", T.wt[:, 256:544], T.win[:, w0 - 16:w0 + 272])
-        runs = [(0, 128, 0, 0), (0, 64, 2, 1), (2, 64, 0, 1), *[(d, 32, d ^ 1, 2) for d in range(4)],
-                *[(d, 32, d ^ 3, 3) for d in range(4)]]
+        got = beside[1](v)
+        runs = [(0, 64, 2, 1), (2, 64, 0, 1), *[(d, 32, d ^ 1, 2) for d in range(4)], *[(d, 32, d ^ 3, 3) for d in range(4)]]
         toks = []
         for i, (d, m, src, j) in enumerate(runs):
-            ab = T.z[32 * d:32 * d + m, j:136:4], T.wt[32 * src:32 * src + m, 0:544:16]
+            ab = T.wt[32 * d:32 * d + m, 4 * j:544:16], T.wt[32 * src:32 * src + m, 0:544:16]
             toks.append(vec("copy", *ab, after=[e]) if i < 5 else act(*ab, F.Copy, after=[e]))
-        beside2()
-        e = vec("scan", T.zs[:], T.rz[:], T.z[:], 0.0, A.mult, A.add, after=[*toks, vrz])
-        return e, vec("ts", out[:], T.zs[:].indirect(T.fo[:, fo:fo + 2]), 256.0, None, A.add, after=[e, vfo])
+        beside[2]()
+        e = vec("scan", T.zs[:], T.rz[:], T.wt[:, 0:544:4], 0.0, A.mult, A.add, after=[*toks, vrz])
+        beside[3]()
+        return got, vec("ts", out[:], T.zs[:].indirect(T.fo[:, fo:fo + 2]), 256.0, None, A.add, after=[e, vfo])
 
     def pick(c_to, s_to, j, c, s, off, *toks, n=K):
         v = vec("copy", c_to[:, j:j + n].bitcast(dt.uint32), c[:].bitcast(dt.uint32).indirect(off), after=toks)
         return v, act(s_to[:, j:j + n], s[:].indirect(off), F.Copy, after=toks)
 
-    vq = vec("quant", T.cx[:, 0:H], T.sx[:, 0:H], T.xb[:, 0:1024], after=[dx[0]])
-    tx, tr0, ts0 = score_half(0, [*vqu, vq])
-    for out, bits in ((T.a48, 48), (T.a2, 2)):
-        vec("ts", out[:], T.ip[:, 0:1], bits, None, A.bitwise_and)
-    vec("ts", T.fo[:, 0:1], T.fx[:], T.fy[:], T.fz[:], A.add, A.add, after=[vf])
-    vfo = vec("ts", T.fo[:, 1:2], T.fx[:], T.fy[:], T.fw[:], A.add, A.add)
-    vval = vec("ts", T.val[:], T.vb[:], T.hc[:], -256.0, A.add, A.add, after=[pvb])
-    sc0 = column(0, tx)
+    def offsets(*which):
+        for i in which:
+            x, w = ((T.fx, T.fz), (T.fx, T.fw), (T.fx, T.fz), (T.fv, T.fu))[i]
+            v = vec("ts", T.fo[:, i:i + 1], x[:], T.fy[:], w[:], A.add, A.add, after=[vf])
+        return v
+
+    t0 = down(0, vu, quantised(0))
+    vqu = (vec("copy", T.cu[:].bitcast(dt.uint32), T.cq[:].bitcast(dt.uint32).indirect(T.u0[:]), after=[vu]),
+           act(T.su[:], T.sq[:].indirect(T.u0[:]), F.Copy, after=[vu]))
+    t1 = down(1, quantised(1))
+    r01 = along(ROW_V[0], 0, 256, *vqu)
+    x1 = along(ROW_S[1], 128, 256)
+    sc0 = column(0, t0)
     th0 = inside(0, sc0)
-    s2 = signs(0, 128, 256, [ts0])
-    vq = vec("quant", T.cx[:, H:2 * H], T.sx[:, H:2 * H], T.xb[:, 1024:2048], after=[dx[1]])
-    tx, tr1, ts1 = score_half(1, [vq])
-    plain(1, 0, 128, 0, [sc0[0], tr0])
-    d = diag(0, 0, th0[0]), diag(1, 128, th0[1])
-    halves(0, 0, d[0], 64)
-    halves(512, 128, d[1])
-    sc1 = column(1, tx)
-    s2 = counted(0, 128, 256, 2, s2)
-    s0 = signs(0, H, 512, [ts1])
+    sc1 = column(1, t1)
     th1 = inside(1, sc1)
-    s1 = signs(1, H, 512, [])
-    s0, s1 = counted(0, H, 512, 0, s0), counted(1, H, 512, 1, s1)
-    for h in (0, 1):
-        srows = act(T.rows[:, H * h:H * h + H], T.ps[:, 512 * (6 + h):512 * (6 + h) + H], F.Copy)
-    plain(2, 0, H, 0, [sc1[0]])
-    plain(3, 0, H, 0)
-    plain(2, 384, 512, 384, [tr1])
-    plain(3, H, 384, H)
-    d = diag(2, H, th1[0]), diag(3, 384, th1[1])
-    row_sum(2, d[0])
-    e = row_sum(3, d[1])
-    vec("ts", T.pou[:, 0:1], T.cs[:, 63:64], T.pl[:, 0:1], T.pl[:, 2:3], A.add, A.add, after=[s0, s2])
+    signs(0, 1, x1)
+    t2 = down(2, quantised(2), sc0[1])
+    x2, r2 = along(ROW_S[2], 256, 384), along(ROW_V[2], 256, 384)
+    sc2 = column(2, t2)
+    sa = signs(0, 2, x2)
+    th2 = inside(2, sc2)
+    sb = signs(1, 2)
+    vfo = offsets(0, 1)
+    vval = vec("ts", T.val[:], T.vb[:], T.hc[:], -256.0, A.add, A.add, after=[pvb])
+    d0 = diag(0, th0, r01)
+    plain(1, 0, 128, sc1[0])
+    t3 = down(3, quantised(3), sc1[1])
+    d1 = diag(1, th1)
+    x3, r3 = along(ROW_S[3], 384, 512), along(ROW_V[3], 384, 512)
+    tall = along(1024, 0, 512, sc2[1])
+    sa = counted(0, 128, 384, 2, sa)
+    sc3 = column(3, t3)
+    s0 = signs(0, 3, x3)
+    th3 = inside(3, sc3)
+    s1 = signs(1, 3)
+    s0, s1 = counted(0, 384, 512, 0, s0), counted(1, 256, 512, 1, s1)
+    srows = act(T.rows[:], T.ps[:, 1024:1536], F.Copy, after=[tall])
+    halves(0, 0, d0, 64)
+    halves(512, 128, d1)
+    plain(2, 0, H, sc2[0])
+    diag(2, th2, r2)
+    d2 = plain(2, 384, 512, r3)
+    plain(3, 0, H, sc3[0])
+    plain(3, H, 384)
+    d3 = diag(3, th3)
+    row_sum(2, d2)
+    e = row_sum(3, d3)
+    vec("ts", T.pou[:, 0:1], T.cs[:, 63:64], T.pl[:, 0:1], T.pl[:, 2:3], A.add, A.add, after=[s0, sa])
     v = vec("ts", T.pou[:, 1:2], T.cs[:, 255:256], T.pl[:, 1:2], None, A.add, after=[s1])
     vpl = vec("ts", T.pou[:, 2:4], T.ce[:, 255:512:256], 256.0, None, A.add, after=[e])
-    zl, ql = to_list((v, vpl), T.val, T.lst, w0, 544, 0)
+
+    def nothing(*toks):
+        return None
+
+    def numbers(tok):
+        return vec("tt", T.nme[:], T.wt[:, 0:256:32], T.wt[:, 16:256:32], A.add, after=[tok])
+
+    vnum, ql = to_list((v, vpl), T.val, T.lst, w0, 544, 0, (nothing, numbers, nothing, nothing))
 
     def send(c, s, j, to, arr, out, pk):
         rid, pid, _ = topo.addr(T.cores[to])
@@ -243,8 +270,7 @@ def rank_program(g, core, T, topo):
         g.remote_dma_fused([tr], local_sem=T.sem["o" + what])
         return {r: ("a%s%d" % (what, r), n) for r in to}, ("o" + what, n)
 
-    snum = act(T.nme[:], T.zs[:, 7:64:8], F.Copy, after=[zl])
-    arrn, outn = note(T.nth[:], T.nme[:], mate, "n", snum)
+    arrn, outn = note(T.nin[:], T.nme[:], mate, "n", vnum)
     s = act(T.sg[:], T.rows[:].indirect(T.lst[:, 16:18]), F.Copy, after=[ql, srows])
     pick(T.c1, T.s1, a0, T.cx, T.sx, T.lst[:, 0:8], ql, n=128)
     vk = vec("tr", T.sgt[:], T.sg[:], after=[s])
@@ -256,15 +282,14 @@ def rank_program(g, core, T, topo):
 
     t = mm(T.ps[:, 0:256], T.cu[:], T.su[:], T.c1[:, a0:a0 + H], T.s1[:, a0:a0 + H], after=p1)
     srv = act(T.rv[:], T.ps[:, 0:256], F.Copy, after=[t])
-    vec("ts", T.fo[:, 2:3], T.fx[:], T.fy[:], T.fz[:], A.add, A.add)
-    vec("ts", T.fw[:], T.a2[:], 4.0, 7.0, A.mult, A.add)
-    vfv = vec("tt", T.fv[:], T.a48[:], T.fx[:], A.add)
-    vk16 = vec("tt", T.k16[:], T.i15[:], T.c16[:], A.add, after=[pc16])
     vec("ts", T.val2[:], T.vb2[:], T.hc[:], None, A.add, after=[pvb2])
-    vec("ts", T.k256[:], T.k16[:], -256.0, None, A.add, after=[vk16])
-    vec("ts", T.fo[:, 3:4], T.fv[:], T.fy[:], T.fw[:], A.add, A.add, after=[vfv])
+    vec("ts", T.k256[:], T.k16[:], -256.0, None, A.add)
+    offsets(2, 3)
     vw = vec("quant", T.cw[:], T.sw[:], T.wb[:], after=[dw])
+    v = vec("tt", T.nab[64:128, :], T.nin[64:128, :], T.nin[0:64, :], A.add, after=[arrn])
     vwin = vec("set", T.win[:, 16:304], 0.0)
+    for d in (64, 96):
+        vec("tt", T.nth[d:d + 32, :], T.nab[64:96, :], T.nab[96:128, :], A.add, after=[v])
 
     def kk(r):
         return T["k%d" % r]
@@ -288,17 +313,17 @@ def rank_program(g, core, T, topo):
         vmsg = vec("ts", msg[:, at:at + 1], T.cs[:, 128 * i + 127:128 * i + 128], T.kb[:, i:i + 1], T.lose[:, i:i + 1],
                    A.add, A.mult, after=[c[i], vl])
     arrm, outm = tell("m", msg[:], vmsg, *smsg)
-
     mine = T.g1[:, 127:128]
     vm1 = vec("scan", T.g1[:], T.f1[:, 0:128], T.f1[:, 128:256], -256.0, A.add, A.add, after=[v])
-    nl, nu = (T.nme, T.nth) if lower else (T.nth, T.nme)
-    vdn = vec("tt", T.dn[:], nu[:], nl[:], A.subtract, after=[arrn, snum])
+    nl, nu = T.zs[64:128, 7:64:8], T.nth[64:128, :]
+    nl, nu = (nl, nu) if lower else (nu, nl)
+    vdn = vec("tt", T.dn[64:128, :], nu, nl, A.subtract)
     v = vec("ts", T.h1[:], T.k256[:], mine, 256.0, A.is_ge, A.mult, after=[vm1])
-    vh = vec("ts", T.h3[:], T.k32[:], mine, None, A.is_ge)
+    vh = vec("ts", T.h3[64:128, :], T.k32[64:128, :], T.g1[64:128, 127:128], None, A.is_ge)
     v = vec("tt", T.h2[:], T.k16[:], T.h1[:], A.add, after=[v])
-    vh = vec("tt", T.h4[:], T.h3[:], T.dn[:], A.mult, after=[vh, vdn])
+    vh = vec("tt", T.h4[64:128, :], T.h3[64:128, :], T.dn[64:128, :], A.mult, after=[vh, vdn])
     vc = vec("copy", T.q1[:], T.h2[:], after=[v])
-    vpn = vec("tt", T.pme[:, 0:8], T.h4[:], nl[:], A.add, after=[vh])
+    vpn = vec("tt", T.pme[64:128, 0:8], T.h4[64:128, :], nl, A.add, after=[vh])
     spn = act(T.pme[:, 8:9], mine, F.Copy, after=[vm1])
     p2 = pick(T.c2, T.s2, H * f2, T.c1, T.s1, T.q1[:], vc, arr1, *p1)
 
@@ -335,8 +360,14 @@ def rank_program(g, core, T, topo):
              A.add, A.add, after=[v, arrm[mate], arrm[other ^ 1]]) for i in range(4)]
     s = replicated(k2, T.pth, arrp)
     ty = products(H * k2, H, 0, arr2)
-    v2 = to_list(e[1::2], T.val2, T.q2, 32, 800, 2, lambda: who(k2, T.pth, arrp), lambda: turned(k2, s))[1]
-    there = [result(*r) for r in ty]
+
+    def half(i):
+        return vec("copy", T.yy[:, 512 + H * k2 + 128 * i:640 + H * k2 + 128 * i], T.ps[:, 512 + 128 * i:640 + 128 * i],
+                   after=[ty[1][2]])
+
+    v2 = to_list(e[1::2], T.val2, T.q2, 32, 800, 2,
+                 (lambda: who(k2, T.pth, arrp), nothing, lambda: turned(k2, s), lambda: half(0)))[1]
+    there = [half(1) if o == 1 else result(*r) for o, r in enumerate(ty[0:3])]
 
     def store(y, out, in_, *toks):
         wait(y, *toks)
@@ -347,12 +378,13 @@ def rank_program(g, core, T, topo):
         toks = [v2, here[o], there[o]]
         return vec("copy", *ab, after=toks) if on_vector else act(*ab, F.Copy, after=toks)
 
-    v = vec("ts", T.idf[:], T.tab[:].indirect(T.q2[:, 16:20]), T.up256[:], None, A.add, after=[v2])
-    store("y", T.id[:], T.idf[0:128:16, :], v)
-    done = [[winners(0, 0, 16, True)], [winners(1, 0, 16, True)], [winners(2, 0, 12, True), winners(2, 12, 16, False)],
-            [winners(3, 0, 16, False)]]
+    done = [[winners(0, 0, 16, True)], [winners(1, 0, 16, False)], [winners(2, 0, 16, True)]]
+    there.append(result(*ty[3]))
+    done.append([winners(3, 0, 4, True), winners(3, 4, 16, False)])
+    v = vec("ts", T.idf[:], T.tab[:].indirect(T.q2[:, 16:20]), T.up256[:], None, A.add)
     for o in range(O):
         store("yyys"[o], T.y[:, K * o:K * o + K], T.ysb[:, K * o:K * o + K], *done[o])
+    store("y", T.id[:], T.idf[0:128:16, :], v)
 
     wait("g", out1, outn, outk, out2, outm, outp, arr1, arr2, arrn, arrp, *arrk.values(), *arrm.values(),
          *[(s, n) for s, n in cnt.items()])

@@ -21,7 +21,7 @@ _bufs("float32", sc4=4, nd=4, th=512, pl=4, vb=64, vb2=64, hc=1, fx=1, fy=1, fz=
       m3=4, lose=2, cp=2, t1=4, idf=64, yy=2048, ysb=1024, fu=1, fv=1, up256=1)
 _bufs("int32", ip=16, i15=16, c16=16, y17=1, a14=1, a112=1, a48=1, a2=1)
 _bufs("uint16", u0=8, pou=4, fo=4, lst=32, q1=16, q2=32)
-SEMAPHORES = ["cv", "ca", "ct", "cp", "du", "dx0", "dx1", "dx2", "dx3", "dw", "dy0", "dy1", "a1", "o1", "on", "ok", "om", "op",
+SEMAPHORES = ["cv", "ca", "ct", "cp", "du", "dx0", "dx1", "dx2", "dx3", "dw", "dy0", "dy1", "a0", "o0", "a1", "o1", "on", "ok", "om", "op",
               "a2", "o2", "an", "ap", "ak0", "ak1", "ak2", "ak3", "am0", "am1", "am2", "am3"]
 STEP, TINY = 1.125 * 2.0 ** -24, 2.0 ** -124
 
@@ -82,18 +82,17 @@ def rank_program(g, core, T, topo):
     wait("g", vneg)
     pdm = inc("cp", g.affine_select(T.dm[:], T.neg[:], [[-1, 128]], A.is_gt if lower else A.is_ge, 0.0, 0, 1))
     pc16 = inc("cp", g.iota(T.c16[:], [[16, 16]], 0, 0))
-    piot = inc("cp", g.iota(T.iot[:], [[1, 256]], -256, 0, **f))
     sg = -1 if lower else 1
-    wait("g", piot)
+    wait("g", pc16)
     for r in range(4):
         run = slice(32 * r, 32 * r + 32)
         inc("cp", g.iota(T.kb[run, :], [[32 * sg, 2]], 64 * r * sg + (255 if lower else 0), sg, **f))
         inc("cp", g.iota(T.k32[run, :], [[32, 8]], -256, 1, **f))
-        p = inc("cp", g.iota(T.vb2[run, :], [[256, 2], [32, 2], [1, 16]], 32 * r - 256, 0, **f))
-    wait("g", p)
+        pvb2 = inc("cp", g.iota(T.vb2[run, :], [[256, 2], [32, 2], [1, 16]], 32 * r - 256, 0, **f))
+    wait("g", pvb2)
+    inc("cp", g.iota(T.iot[0:64, :], [[1, 256]], -256, 0, **f))
     inc("cp", g.iota(T.up256[0:64, :], [[0, 1]], 0, 0, **f))
     inc("cp", g.iota(T.up256[64:128, :], [[0, 1]], 256, 0, **f))
-    pvb2 = inc("cp", g.iota(T.rep[64:128, :], [[0, 512]], 0, 0, **f))
     w0 = 32 if lower else 32 + H
     vec("set", T.up[:, 8:512], 0.0)
     vec("set", T.u0[:], 0)
@@ -203,36 +202,35 @@ def rank_program(g, core, T, topo):
     t2 = down(2, quantised(2), sc0[1])
     x2, r2 = along(ROW_S[2], 256, 384), along(ROW_V[2], 256, 384)
     sc2 = column(2, t2)
-    sa = signs(0, 2, x2)
+    signs(0, 2, x2)
     th2 = inside(2, sc2)
-    sb = signs(1, 2)
     vfo = offsets(0, 1)
     vval = vec("ts", T.val[:], T.vb[:], T.hc[:], -256.0, A.add, A.add, after=[pvb])
-    d0 = diag(0, th0, r01)
+    diag(0, th0, r01)
     plain(1, 0, 128, sc1[0])
     t3 = down(3, quantised(3), sc1[1])
-    d1 = diag(1, th1)
+    diag(1, th1)
     x3, r3 = along(ROW_S[3], 384, 512), along(ROW_V[3], 384, 512)
     tall = along(1024, 0, 512, sc2[1])
-    sa = counted(0, 128, 384, 2, sa)
     sc3 = column(3, t3)
     s0 = signs(0, 3, x3)
     th3 = inside(3, sc3)
     s1 = signs(1, 3)
-    s0, s1 = counted(0, 384, 512, 0, s0), counted(1, 256, 512, 1, s1)
+    s0, s1 = counted(0, 128, 512, 0, s0), counted(1, 384, 512, 1, s1)
     srows = act(T.rows[:], T.ps[:, 1024:1536], F.Copy, after=[tall])
-    halves(0, 0, d0, 64)
-    halves(512, 128, d1)
+    plain(1, H, 384, r2)
     plain(2, 0, H, sc2[0])
-    diag(2, th2, r2)
+    diag(2, th2)
     d2 = plain(2, 384, 512, r3)
     plain(3, 0, H, sc3[0])
     plain(3, H, 384)
     d3 = diag(3, th3)
+    halves(0, 0, d2, 64)
+    v = vec("scan", T.cs[:, 64:256], T.fl[:, 512:704], T.fl[:, 704:896], -128.0, A.add, A.add)
     row_sum(2, d2)
     e = row_sum(3, d3)
-    vec("ts", T.pou[:, 0:1], T.cs[:, 63:64], T.pl[:, 0:1], T.pl[:, 2:3], A.add, A.add, after=[s0, sa])
-    v = vec("ts", T.pou[:, 1:2], T.cs[:, 255:256], T.pl[:, 1:2], None, A.add, after=[s1])
+    vec("ts", T.pou[:, 0:1], T.cs[:, 63:64], T.pl[:, 0:1], None, A.add, after=[s0, v])
+    v = vec("ts", T.pou[:, 1:2], T.cs[:, 255:256], T.pl[:, 1:2], 128.0, A.add, A.add, after=[s1])
     vpl = vec("ts", T.pou[:, 2:4], T.ce[:, 255:512:256], 256.0, None, A.add, after=[e])
 
     def nothing(*toks):
@@ -243,16 +241,6 @@ def rank_program(g, core, T, topo):
 
     vnum, ql = to_list((v, vpl), T.val, T.lst, w0, 544, 0, (nothing, numbers, nothing, nothing))
 
-    def send(c, s, j, to, arr, out, pk):
-        rid, pid, _ = topo.addr(T.cores[to])
-        m, n = topo.mask(core, T.cores[to]), len(topo.engines(core, T.cores[to]))
-        wait("g", pk[0])
-        cc = c[:, j:j + K].bitcast(dt.uint8)
-        g.remote_dma(cc, cc, T.sem[arr], T.sem[out], pid, rid, m)
-        wait("g", pk[1])
-        g.remote_dma(s[:, j:j + K], s[:, j:j + K], T.sem[arr], T.sem[out], pid, rid, m)
-        return (arr, 2 * n), (out, 2 * n)
-
     def note(dst, src, to, what, *toks):
         rid, pid, _ = topo.addr(T.cores[to])
         wait("g", *toks)
@@ -260,8 +248,7 @@ def rank_program(g, core, T, topo):
         n = len(topo.engines(core, T.cores[to]))
         return ("a" + what, n), ("o" + what, n)
 
-    def tell(what, me, *toks):
-        to = (other, other ^ 1, mate)
+    def tell(what, me, to, *toks):
         m, n = topo.mask(core, T.cores[other]), len(topo.engines(core, T.cores[other]))
         ids = [DstId(rid=topo.addr(T.cores[r])[0], pnc=topo.addr(T.cores[r])[1]) for r in to]
         tr = RemoteDMATransfer(dst_ids=ids, dma_engine_mask=m, remote_sem=T.sem["a%s%d" % (what, rank)], src=me,
@@ -272,13 +259,17 @@ def rank_program(g, core, T, topo):
 
     arrn, outn = note(T.nin[:], T.nme[:], mate, "n", vnum)
     s = act(T.sg[:], T.rows[:].indirect(T.lst[:, 16:18]), F.Copy, after=[ql, srows])
-    pick(T.c1, T.s1, a0, T.cx, T.sx, T.lst[:, 0:8], ql, n=128)
+    p0 = pick(T.c1, T.s1, a0, T.cx, T.sx, T.lst[:, 0:8], ql, n=128)
     vk = vec("tr", T.sgt[:], T.sg[:], after=[s])
     kme = T.sgt[:, 15:17]
-    arrk, outk = tell("k", kme, vk)
+    arrk, outk = tell("k", kme, (mate, other, other ^ 1), vk)
 
     p1 = pick(T.c1, T.s1, a0 + 128, T.cx, T.sx, T.lst[:, 8:16], ql, n=128)
-    arr1, out1 = send(T.c1, T.s1, a0, mate, "a1", "o1", p1)
+    cc = [T.c1[:, a0 + 128 * i:a0 + 128 * i + 128].bitcast(dt.uint8) for i in (0, 1)]
+    note(cc[0], cc[0], mate, "0", p0[0])
+    arr0, out0 = [(s, 2 * n) for s, n in note(T.s1[:, a0:a0 + K], T.s1[:, a0:a0 + K], mate, "0", p1[1])]
+    arr1, out1 = note(cc[1], cc[1], mate, "1", p1[0])
+    piot = inc("cp", g.iota(T.rep[64:128, :], [[0, 512]], 0, 0, **f))
 
     t = mm(T.ps[:, 0:256], T.cu[:], T.su[:], T.c1[:, a0:a0 + H], T.s1[:, a0:a0 + H], after=p1)
     srv = act(T.rv[:], T.ps[:, 0:256], F.Copy, after=[t])
@@ -289,50 +280,60 @@ def rank_program(g, core, T, topo):
     v = vec("tt", T.nab[64:128, :], T.nin[64:128, :], T.nin[0:64, :], A.add, after=[arrn])
     vwin = vec("set", T.win[:, 16:304], 0.0)
     for d in (64, 96):
-        vec("tt", T.nth[d:d + 32, :], T.nab[64:96, :], T.nab[96:128, :], A.add, after=[v])
+        v = vec("tt", T.nth[d:d + 32, :], T.nab[64:96, :], T.nab[96:128, :], A.add, after=[v] if d == 64 else [])
+    nl, nu = T.zs[64:128, 7:64:8], T.nth[64:128, :]
+    nl, nu = (nl, nu) if lower else (nu, nl)
 
     def kk(r):
         return T["k%d" % r]
 
     msg = T["m%d" % rank]
+
+    def ahead(i):
+        return vec("ts", T.fl[:, 1024 + H * i:1280 + H * i], T.rv[:], kk(mate)[:, i:i + 1], None, A.is_ge if lower else A.is_gt,
+                   after=[arrk[mate], srv])
+
+    c = [ahead(0)]
     vcp = vec("tt", T.cp[:], kk(other)[:], kk(other ^ 1)[:], A.max, after=[arrk[other], arrk[other ^ 1]])
     s = [act(T.fl[:, H * i:H * i + H], T.rv[:], F.Sign, scale=-1.0, bias=T.cp[:, i:i + 1], after=[vcp, srv]) for i in (0, 1)]
     how = (F.Sign, 1.0) if f2 == 0 else (F.Relu, 0.0)
     smsg = [act(T.fl[:, 512 + H * i:768 + H * i], T.fl[:, H * i:H * i + H], how[0], scale=-1.0, bias=how[1],
                 accum_out=msg[:, 2 * k2 + i:2 * k2 + i + 1], after=[s[i]]) for i in (0, 1)]
-    c = [vec("ts", T.fl[:, 1024 + H * i:1280 + H * i], T.rv[:], kk(mate)[:, i:i + 1], None, A.is_ge if lower else A.is_gt,
-             after=[arrk[mate], srv]) for i in (0, 1)]
+    c.append(ahead(1))
+    for i, arr in enumerate((arr0, arr1)):
+        j, theirs = b0 + 128 * i, T.ps[:, 512 * (1 + i):512 * (1 + i) + 128]
+        row = mm(theirs, T.cu[:], T.su[:], T.c1[:, j:j + 128], T.s1[:, j:j + 128], after=[arr, srows])
+        rows = T.rv[:, 128 * i:128 * i + 128], theirs
+        v = vec("tt", T.f1[:, 128 * i:128 * i + 128], *(rows if lower else rows[::-1]), A.is_ge, after=[row])
     vl = vec("tt", T.lose[:], kme, kk(mate)[:], A.is_lt if lower else A.is_le)
     c = [halves(1024 + H * i, 128 * i, c[i]) for i in (0, 1)]
-    row = mm(T.ps[:, 512:768], T.cu[:], T.su[:], T.c1[:, b0:b0 + H], T.s1[:, b0:b0 + H], after=[arr1])
-    theirs = T.ps[:, 512:768]
-    rows = (T.rv[:], theirs) if lower else (theirs, T.rv[:])
-    v = vec("tt", T.f1[:], rows[0], rows[1], A.is_ge, after=[row])
+    mine = T.g1[:, 127:128]
+    vm1 = vec("scan", T.g1[:], T.f1[:, 0:128], T.f1[:, 128:256], -256.0, A.add, A.add, after=[v])
     for i in (0, 1):
         at = 2 * f2 + i
         vmsg = vec("ts", msg[:, at:at + 1], T.cs[:, 128 * i + 127:128 * i + 128], T.kb[:, i:i + 1], T.lose[:, i:i + 1],
                    A.add, A.mult, after=[c[i], vl])
-    arrm, outm = tell("m", msg[:], vmsg, *smsg)
-    mine = T.g1[:, 127:128]
-    vm1 = vec("scan", T.g1[:], T.f1[:, 0:128], T.f1[:, 128:256], -256.0, A.add, A.add, after=[v])
-    nl, nu = T.zs[64:128, 7:64:8], T.nth[64:128, :]
-    nl, nu = (nl, nu) if lower else (nu, nl)
-    vdn = vec("tt", T.dn[64:128, :], nu, nl, A.subtract)
+    arrm, outm = tell("m", msg[:], (other, other ^ 1, mate), vmsg, *smsg)
     v = vec("ts", T.h1[:], T.k256[:], mine, 256.0, A.is_ge, A.mult, after=[vm1])
+    vec("tt", T.dn[64:128, :], nu, nl, A.subtract)
     vh = vec("ts", T.h3[64:128, :], T.k32[64:128, :], T.g1[64:128, 127:128], None, A.is_ge)
     v = vec("tt", T.h2[:], T.k16[:], T.h1[:], A.add, after=[v])
-    vh = vec("tt", T.h4[64:128, :], T.h3[64:128, :], T.dn[64:128, :], A.mult, after=[vh, vdn])
+    vh = vec("tt", T.h4[64:128, :], T.h3[64:128, :], T.dn[64:128, :], A.mult, after=[vh])
     vc = vec("copy", T.q1[:], T.h2[:], after=[v])
     vpn = vec("tt", T.pme[64:128, 0:8], T.h4[64:128, :], nl, A.add, after=[vh])
     spn = act(T.pme[:, 8:9], mine, F.Copy, after=[vm1])
-    p2 = pick(T.c2, T.s2, H * f2, T.c1, T.s1, T.q1[:], vc, arr1, *p1)
+    j = H * f2
+    p2 = pick(T.c2, T.s2, j, T.c1, T.s1, T.q1[:], vc, arr0, arr1, *p1)
 
     arrp, outp = note(T.pth[:, 0:9], T.pme[:, 0:9], other, "p", vpn, spn)
-    arr2, out2 = send(T.c2, T.s2, H * f2, other, "a2", "o2", p2)
+    cc = T.c2[:, j:j + K].bitcast(dt.uint8)
+    note(cc, cc, other, "2", p2[0])
+    arr2, out2 = [(s, 2 * n) for s, n in note(T.s2[:, j:j + K], T.s2[:, j:j + K], other, "2", p2[1])]
+
 
     def replicated(h, src, *toks):
         for j in (0, 16):
-            s = act(T.rep[64:128, H * h + j:H * h + H:32], src[64:128, 0:8], F.Copy, after=toks)
+            s = act(T.rep[64:128, H * h + j:H * h + H:32], src[64:128, 0:8], F.Copy, after=[piot, *toks])
         return s
 
     def who(h, m, *toks):
@@ -352,22 +353,21 @@ def rank_program(g, core, T, topo):
 
     sme = replicated(f2, T.pme, vpn)
     who(f2, T.pme, spn)
-    turned(f2, sme)
     here = [result(*r) for r in products(H * f2, H, 4, vw, *p2)]
 
     v = vec("tt", T.t1[:], msg[:], T["m%d" % other][:], A.add, after=[*smsg, arrm[other]])
     e = [vec("ts", T.pou[:, i:i + 1], T.t1[:, i:i + 1], T["m%d" % mate][:, i:i + 1], T["m%d" % (other ^ 1)][:, i:i + 1],
              A.add, A.add, after=[v, arrm[mate], arrm[other ^ 1]]) for i in range(4)]
-    s = replicated(k2, T.pth, arrp)
     ty = products(H * k2, H, 0, arr2)
 
     def half(i):
         return vec("copy", T.yy[:, 512 + H * k2 + 128 * i:640 + H * k2 + 128 * i], T.ps[:, 512 + 128 * i:640 + 128 * i],
                    after=[ty[1][2]])
 
+    s = replicated(k2, T.pth, arrp)
     v2 = to_list(e[1::2], T.val2, T.q2, 32, 800, 2,
-                 (lambda: who(k2, T.pth, arrp), nothing, lambda: turned(k2, s), lambda: half(0)))[1]
-    there = [half(1) if o == 1 else result(*r) for o, r in enumerate(ty[0:3])]
+                 (lambda: turned(f2, sme), lambda tok: who(k2, T.pth, arrp), lambda: turned(k2, s), lambda: half(0)))[1]
+    there = [half(1) if o == 1 else result(*r) for o, r in enumerate(ty)]
 
     def store(y, out, in_, *toks):
         wait(y, *toks)
@@ -378,13 +378,11 @@ def rank_program(g, core, T, topo):
         toks = [v2, here[o], there[o]]
         return vec("copy", *ab, after=toks) if on_vector else act(*ab, F.Copy, after=toks)
 
-    done = [[winners(0, 0, 16, True)], [winners(1, 0, 16, False)], [winners(2, 0, 16, True)]]
-    there.append(result(*ty[3]))
-    done.append([winners(3, 0, 4, True), winners(3, 4, 16, False)])
+    done = [winners(o, 0, 16, o < 2) for o in range(O)]
     v = vec("ts", T.idf[:], T.tab[:].indirect(T.q2[:, 16:20]), T.up256[:], None, A.add)
-    for o in range(O):
-        store("yyys"[o], T.y[:, K * o:K * o + K], T.ysb[:, K * o:K * o + K], *done[o])
+    for o in (0, 2, 1, 3):
+        store("yyys"[o], T.y[:, K * o:K * o + K], T.ysb[:, K * o:K * o + K], done[o])
     store("y", T.id[:], T.idf[0:128:16, :], v)
 
-    wait("g", out1, outn, outk, out2, outm, outp, arr1, arr2, arrn, arrp, *arrk.values(), *arrm.values(),
+    wait("g", out0, out1, outn, outk, out2, outm, outp, arr0, arr1, arr2, arrn, arrp, *arrk.values(), *arrm.values(),
          *[(s, n) for s, n in cnt.items()])

@@ -11,18 +11,18 @@ def _bufs(dtype, **widths):
         SCRATCH[name] = ("sbuf", [128, n], dtype)
 
 
-_bufs("float8_e4m3fn_x4", cx=512, cq=128, cu=128, cw=512, c1=512, c2=512, c3=256)
-_bufs("uint8", sx=512, sq=128, su=128, sw=512, s1=512, s2=512, s3=256)
+_bufs("float8_e4m3fn_x4", cx=512, cq=128, cu=128, cw=512, c1=512, c2=512)
+_bufs("uint8", sx=512, sq=128, su=128, sw=512, s1=512, s2=512)
 _bufs("bfloat16", xb=2048, wb=2048, up=512, neg=128, dm=128, fl=2048, cs=256, ce=512, f1=256, g1=128,
       val=64, val2=64, win=800, wt=544, zs=136, rz=136, iot=256, rep=512, tab=512,
       nme=8, nin=8, nab=8, nth=8, pme=16, pth=16)
 _bufs("float32", sc4=4, nd=4, th=512, pl=4, vb=64, vb2=64, hc=1, fx=1, fy=1, fz=1, fw=1, k16=16, k256=16, kb=2,
       k32=8, rv=256, rows=512, sg=32, sgt=32, h1=16, h2=16, dn=8, h3=8, h4=8, k0=2, k1=2, k2=2, k3=2, m0=4, m1=4, m2=4,
-      m3=4, lose=2, cp=2, t1=4, idf=64, yy=2048, ysb=1024, fu=1, fv=1, up256=1)
+      m3=4, mb=512, cp=2, t1=4, idf=64, yy=2048, ysb=1024, fu=1, fv=1, up256=1)
 _bufs("int32", ip=16, i15=16, c16=16, y17=1, a14=1, a112=1, a48=1, a2=1)
 _bufs("uint16", u0=8, pou=4, fo=4, lst=32, q1=16, q2=32)
-SEMAPHORES = ["cv", "ca", "ct", "cp", "du", "dx0", "dx1", "dx2", "dx3", "dw", "dy0", "dy1", "a0", "o0", "a1", "o1", "on", "ok", "om", "op",
-              "a2", "o2", "an", "ap", "ak0", "ak1", "ak2", "ak3", "am0", "am1", "am2", "am3"]
+SEMAPHORES = ["cv", "ca", "ct", "cp", "du", "dx0", "dx1", "dx2", "dx3", "dw", "dy0", "dy1", "a0", "o0", "a1", "o1", "a2", "o2",
+              "on", "ok", "om", "op", "an", "ap", "ak0", "ak1", "ak2", "ak3", "am0", "am1", "am2", "am3"]
 STEP, TINY = 1.125 * 2.0 ** -24, 2.0 ** -124
 
 
@@ -92,14 +92,14 @@ def rank_program(g, core, T, topo):
     wait("g", pvb2)
     inc("cp", g.iota(T.iot[0:64, :], [[1, 256]], -256, 0, **f))
     inc("cp", g.iota(T.up256[0:64, :], [[0, 1]], 0, 0, **f))
-    inc("cp", g.iota(T.up256[64:128, :], [[0, 1]], 256, 0, **f))
+    piot = inc("cp", g.iota(T.up256[64:128, :], [[0, 1]], 256, 0, **f))
     w0 = 32 if lower else 32 + H
     vec("set", T.up[:, 8:512], 0.0)
     vec("set", T.u0[:], 0)
     vec("set", T.pme[0:64, :], 0.0)
     v1 = vec("set", T.rz[:], 1.0)
     vwin = vec("set", T.win[:, w0 - 16:w0 + 272], 0.0)
-    v15 = vec("ts", T.i15[:], T.ip[:], 15, None, A.bitwise_and, after=[pip])
+    vec("ts", T.i15[:], T.ip[:], 15, None, A.bitwise_and, after=[pip])
     for out, bits in ((T.y17, 17), (T.a14, 14), (T.a112, 112), (T.a48, 48), (T.a2, 2)):
         va = vec("ts", out[:], T.ip[:, 0:1], bits, None, A.bitwise_and)
     vrz = vec("set", T.rz[:, 0:136:8], 0.0, after=[v1])
@@ -155,8 +155,8 @@ def rank_program(g, core, T, topo):
         return vec("tt", T.fl[:, 640 * t:640 * t + 128], T.ps[:, ROW_V[t]:ROW_V[t] + 128], T.th[:, 128 * t:128 * t + 128],
                    A.is_gt if lower else A.is_le, after=toks)
 
-    def halves(z, j, tok, n=128):
-        return vec("scan", T.cs[:, j:j + n], T.fl[:, z:z + n], T.fl[:, z + n:z + 2 * n], 0.0, A.add, A.add, after=[tok])
+    def halves(z, j, tok, n, start=0.0):
+        return vec("scan", T.cs[:, j:j + n], T.fl[:, z:z + n], T.fl[:, z + n:z + 2 * n], start, A.add, A.add, after=[tok])
 
     def row_sum(t, tok):
         z, j = 512 * t, 256 * (t % 2)
@@ -172,11 +172,11 @@ def rank_program(g, core, T, topo):
         toks = []
         for i, (d, m, src, j) in enumerate(runs):
             ab = T.wt[32 * d:32 * d + m, 4 * j:544:16], T.wt[32 * src:32 * src + m, 0:544:16]
-            toks.append(vec("copy", *ab, after=[e]) if i < 5 else act(*ab, F.Copy, after=[e]))
+            toks.append(vec("copy", *ab, after=[e]) if i < 6 else act(*ab, F.Copy, after=[e]))
         beside[2]()
         e = vec("scan", T.zs[:], T.rz[:], T.wt[:, 0:544:4], 0.0, A.mult, A.add, after=[*toks, vrz])
         beside[3]()
-        return got, vec("ts", out[:], T.zs[:].indirect(T.fo[:, fo:fo + 2]), 256.0, None, A.add, after=[e, vfo])
+        return got, vec("ts", out[:, 0:16 * fo], T.zs[:].indirect(T.fo[:, 0:fo]), 256.0, None, A.add, after=[e, vfo])
 
     def pick(c_to, s_to, j, c, s, off, *toks, n=K):
         v = vec("copy", c_to[:, j:j + n].bitcast(dt.uint32), c[:].bitcast(dt.uint32).indirect(off), after=toks)
@@ -184,49 +184,48 @@ def rank_program(g, core, T, topo):
 
     def offsets(*which):
         for i in which:
-            x, w = ((T.fx, T.fz), (T.fx, T.fw), (T.fx, T.fz), (T.fv, T.fu))[i]
+            x, w = ((T.fx, T.fz), (T.fx, T.fw), (T.fv, T.fu))[i]
             v = vec("ts", T.fo[:, i:i + 1], x[:], T.fy[:], w[:], A.add, A.add, after=[vf])
         return v
 
     t0 = down(0, vu, quantised(0))
-    vqu = (vec("copy", T.cu[:].bitcast(dt.uint32), T.cq[:].bitcast(dt.uint32).indirect(T.u0[:]), after=[vu]),
-           act(T.su[:], T.sq[:].indirect(T.u0[:]), F.Copy, after=[vu]))
+    vqu = pick(T.cu, T.su, 0, T.cq, T.sq, T.u0[:], vu, n=128)
     t1 = down(1, quantised(1))
     r01 = along(ROW_V[0], 0, 256, *vqu)
-    x1 = along(ROW_S[1], 128, 256)
     sc0 = column(0, t0)
     th0 = inside(0, sc0)
     sc1 = column(1, t1)
-    th1 = inside(1, sc1)
-    signs(0, 1, x1)
     t2 = down(2, quantised(2), sc0[1])
-    x2, r2 = along(ROW_S[2], 256, 384), along(ROW_V[2], 256, 384)
-    sc2 = column(2, t2)
-    signs(0, 2, x2)
-    th2 = inside(2, sc2)
+    x1 = along(ROW_S[1], 128, 256)
+    r2, x2 = along(ROW_V[2], 256, 384), along(ROW_S[2], 256, 384)
     vfo = offsets(0, 1)
     vval = vec("ts", T.val[:], T.vb[:], T.hc[:], -256.0, A.add, A.add, after=[pvb])
-    diag(0, th0, r01)
-    plain(1, 0, 128, sc1[0])
     t3 = down(3, quantised(3), sc1[1])
-    diag(1, th1)
-    x3, r3 = along(ROW_S[3], 384, 512), along(ROW_V[3], 384, 512)
+    r3, x3 = along(ROW_V[3], 384, 512), along(ROW_S[3], 384, 512)
+    sc2 = column(2, t2)
     tall = along(1024, 0, 512, sc2[1])
+    th1 = inside(1, sc1)
+    signs(0, 1, x1)
+    th2 = inside(2, sc2)
     sc3 = column(3, t3)
+    signs(0, 2, x2)
     s0 = signs(0, 3, x3)
     th3 = inside(3, sc3)
     s1 = signs(1, 3)
     s0, s1 = counted(0, 128, 512, 0, s0), counted(1, 384, 512, 1, s1)
     srows = act(T.rows[:], T.ps[:, 1024:1536], F.Copy, after=[tall])
-    plain(1, H, 384, r2)
+    d0 = diag(0, th0, r01)
+    plain(1, 0, 128, sc1[0])
+    halves(0, 0, d0, 64)
     plain(2, 0, H, sc2[0])
-    diag(2, th2)
-    d2 = plain(2, 384, 512, r3)
+    diag(1, th1)
+    d1 = plain(1, H, 384, r2)
+    plain(2, 384, 512, r3)
+    d2 = diag(2, th2)
     plain(3, 0, H, sc3[0])
     plain(3, H, 384)
     d3 = diag(3, th3)
-    halves(0, 0, d2, 64)
-    v = vec("scan", T.cs[:, 64:256], T.fl[:, 512:704], T.fl[:, 704:896], -128.0, A.add, A.add)
+    v = halves(512, 64, d1, 192, -128.0)
     row_sum(2, d2)
     e = row_sum(3, d3)
     vec("ts", T.pou[:, 0:1], T.cs[:, 63:64], T.pl[:, 0:1], None, A.add, after=[s0, v])
@@ -239,7 +238,7 @@ def rank_program(g, core, T, topo):
     def numbers(tok):
         return vec("tt", T.nme[:], T.wt[:, 0:256:32], T.wt[:, 16:256:32], A.add, after=[tok])
 
-    vnum, ql = to_list((v, vpl), T.val, T.lst, w0, 544, 0, (nothing, numbers, nothing, nothing))
+    vnum, ql = to_list((v, vpl), T.val, T.lst, w0, 544, 2, (nothing, numbers, nothing, nothing))
 
     def note(dst, src, to, what, *toks):
         rid, pid, _ = topo.addr(T.cores[to])
@@ -252,7 +251,7 @@ def rank_program(g, core, T, topo):
         m, n = topo.mask(core, T.cores[other]), len(topo.engines(core, T.cores[other]))
         ids = [DstId(rid=topo.addr(T.cores[r])[0], pnc=topo.addr(T.cores[r])[1]) for r in to]
         tr = RemoteDMATransfer(dst_ids=ids, dma_engine_mask=m, remote_sem=T.sem["a%s%d" % (what, rank)], src=me,
-                               dsts=[T["%s%d" % (what, rank)][:]] * 3)
+                               dsts=[T["%s%d" % (what, rank)][:]] * len(to))
         wait("g", *toks)
         g.remote_dma_fused([tr], local_sem=T.sem["o" + what])
         return {r: ("a%s%d" % (what, r), n) for r in to}, ("o" + what, n)
@@ -262,126 +261,131 @@ def rank_program(g, core, T, topo):
     p0 = pick(T.c1, T.s1, a0, T.cx, T.sx, T.lst[:, 0:8], ql, n=128)
     vk = vec("tr", T.sgt[:], T.sg[:], after=[s])
     kme = T.sgt[:, 15:17]
-    arrk, outk = tell("k", kme, (mate, other, other ^ 1), vk)
 
-    p1 = pick(T.c1, T.s1, a0 + 128, T.cx, T.sx, T.lst[:, 8:16], ql, n=128)
     cc = [T.c1[:, a0 + 128 * i:a0 + 128 * i + 128].bitcast(dt.uint8) for i in (0, 1)]
     note(cc[0], cc[0], mate, "0", p0[0])
+    arrk, outk = tell("k", kme, (other, other ^ 1, mate), vk)
+    p1 = pick(T.c1, T.s1, a0 + 128, T.cx, T.sx, T.lst[:, 8:16], ql, n=128)
     arr0, out0 = [(s, 2 * n) for s, n in note(T.s1[:, a0:a0 + K], T.s1[:, a0:a0 + K], mate, "0", p1[1])]
     arr1, out1 = note(cc[1], cc[1], mate, "1", p1[0])
-    piot = inc("cp", g.iota(T.rep[64:128, :], [[0, 512]], 0, 0, **f))
+    prep = inc("cp", g.iota(T.rep[64:128, :], [[0, 512]], 0, 0, **f))
 
     t = mm(T.ps[:, 0:256], T.cu[:], T.su[:], T.c1[:, a0:a0 + H], T.s1[:, a0:a0 + H], after=p1)
     srv = act(T.rv[:], T.ps[:, 0:256], F.Copy, after=[t])
     vec("ts", T.val2[:], T.vb2[:], T.hc[:], None, A.add, after=[pvb2])
     vec("ts", T.k256[:], T.k16[:], -256.0, None, A.add)
-    offsets(2, 3)
+    offsets(2)
     vw = vec("quant", T.cw[:], T.sw[:], T.wb[:], after=[dw])
     v = vec("tt", T.nab[64:128, :], T.nin[64:128, :], T.nin[0:64, :], A.add, after=[arrn])
     vwin = vec("set", T.win[:, 16:304], 0.0)
     for d in (64, 96):
-        v = vec("tt", T.nth[d:d + 32, :], T.nab[64:96, :], T.nab[96:128, :], A.add, after=[v] if d == 64 else [])
+        vec("tt", T.nth[d:d + 32, :], T.nab[64:96, :], T.nab[96:128, :], A.add, after=[v])
     nl, nu = T.zs[64:128, 7:64:8], T.nth[64:128, :]
     nl, nu = (nl, nu) if lower else (nu, nl)
 
     def kk(r):
         return T["k%d" % r]
 
-    msg = T["m%d" % rank]
+    def who(h, m, *toks):
+        return vec("ts", T.tab[0:64, H * h:H * h + H], T.iot[0:64, :], m, 2.0 * h, A.is_ge, A.add, after=[piot, *toks])
 
-    def ahead(i):
-        return vec("ts", T.fl[:, 1024 + H * i:1280 + H * i], T.rv[:], kk(mate)[:, i:i + 1], None, A.is_ge if lower else A.is_gt,
-                   after=[arrk[mate], srv])
-
-    c = [ahead(0)]
+    msg = T.mb[:, 508:512]
     vcp = vec("tt", T.cp[:], kk(other)[:], kk(other ^ 1)[:], A.max, after=[arrk[other], arrk[other ^ 1]])
     s = [act(T.fl[:, H * i:H * i + H], T.rv[:], F.Sign, scale=-1.0, bias=T.cp[:, i:i + 1], after=[vcp, srv]) for i in (0, 1)]
     how = (F.Sign, 1.0) if f2 == 0 else (F.Relu, 0.0)
     smsg = [act(T.fl[:, 512 + H * i:768 + H * i], T.fl[:, H * i:H * i + H], how[0], scale=-1.0, bias=how[1],
-                accum_out=msg[:, 2 * k2 + i:2 * k2 + i + 1], after=[s[i]]) for i in (0, 1)]
-    c.append(ahead(1))
+                accum_out=T.mb[:, 508 + 2 * k2 + i:509 + 2 * k2 + i], after=[s[i]]) for i in (0, 1)]
+    c = [vec("ts", T.fl[:, 1024 + H * i:1280 + H * i], T.rv[:], kk(mate)[:, i:i + 1], None, A.is_ge if lower else A.is_gt,
+             after=[arrk[mate], srv]) for i in (0, 1)]
+
     for i, arr in enumerate((arr0, arr1)):
         j, theirs = b0 + 128 * i, T.ps[:, 512 * (1 + i):512 * (1 + i) + 128]
         row = mm(theirs, T.cu[:], T.su[:], T.c1[:, j:j + 128], T.s1[:, j:j + 128], after=[arr, srows])
         rows = T.rv[:, 128 * i:128 * i + 128], theirs
         v = vec("tt", T.f1[:, 128 * i:128 * i + 128], *(rows if lower else rows[::-1]), A.is_ge, after=[row])
-    vl = vec("tt", T.lose[:], kme, kk(mate)[:], A.is_lt if lower else A.is_le)
-    c = [halves(1024 + H * i, 128 * i, c[i]) for i in (0, 1)]
+
+    def place(i):
+        z = 1024 + H * i
+        return vec("scan", T.mb[:, 2 * f2 + i:512:4], T.fl[:, z:z + 128], T.fl[:, z + 128:z + 256], T.kb[:, i:i + 1],
+                   A.add, A.add, after=[c[i]])
+
+    place(0)
     mine = T.g1[:, 127:128]
     vm1 = vec("scan", T.g1[:], T.f1[:, 0:128], T.f1[:, 128:256], -256.0, A.add, A.add, after=[v])
-    for i in (0, 1):
-        at = 2 * f2 + i
-        vmsg = vec("ts", msg[:, at:at + 1], T.cs[:, 128 * i + 127:128 * i + 128], T.kb[:, i:i + 1], T.lose[:, i:i + 1],
-                   A.add, A.mult, after=[c[i], vl])
-    arrm, outm = tell("m", msg[:], (other, other ^ 1, mate), vmsg, *smsg)
+    arrm, outm = tell("m", msg, (mate, other, other ^ 1), place(1), *smsg)
     v = vec("ts", T.h1[:], T.k256[:], mine, 256.0, A.is_ge, A.mult, after=[vm1])
     vec("tt", T.dn[64:128, :], nu, nl, A.subtract)
     vh = vec("ts", T.h3[64:128, :], T.k32[64:128, :], T.g1[64:128, 127:128], None, A.is_ge)
     v = vec("tt", T.h2[:], T.k16[:], T.h1[:], A.add, after=[v])
+    who(f2, T.g1[0:64, 127:128])
     vh = vec("tt", T.h4[64:128, :], T.h3[64:128, :], T.dn[64:128, :], A.mult, after=[vh])
     vc = vec("copy", T.q1[:], T.h2[:], after=[v])
+    vec("copy", T.pme[:, 8:9], mine)
     vpn = vec("tt", T.pme[64:128, 0:8], T.h4[64:128, :], nl, A.add, after=[vh])
-    spn = act(T.pme[:, 8:9], mine, F.Copy, after=[vm1])
     j = H * f2
     p2 = pick(T.c2, T.s2, j, T.c1, T.s1, T.q1[:], vc, arr0, arr1, *p1)
 
-    arrp, outp = note(T.pth[:, 0:9], T.pme[:, 0:9], other, "p", vpn, spn)
+    arrp, outp = note(T.pth[:, 0:9], T.pme[:, 0:9], other, "p", vpn)
     cc = T.c2[:, j:j + K].bitcast(dt.uint8)
     note(cc, cc, other, "2", p2[0])
     arr2, out2 = [(s, 2 * n) for s, n in note(T.s2[:, j:j + K], T.s2[:, j:j + K], other, "2", p2[1])]
 
-
     def replicated(h, src, *toks):
         for j in (0, 16):
-            s = act(T.rep[64:128, H * h + j:H * h + H:32], src[64:128, 0:8], F.Copy, after=[piot, *toks])
+            s = vec("copy", T.rep[64:128, H * h + j:H * h + H:32], src[64:128, 0:8], after=[prep, *toks])
         return s
-
-    def who(h, m, *toks):
-        return vec("ts", T.tab[0:64, H * h:H * h + H], T.iot[0:64, :], m[0:64, 8:9], 2.0 * h, A.is_ge, A.add,
-                   after=[piot, *toks])
 
     def turned(h, tok):
         return vec("tr", T.tab[64:128, H * h:H * h + H], T.rep[64:128, H * h:H * h + H], after=[tok])
 
     def products(j, n, b, *toks):
-        ty = [mm(T.ps[:, 512 * (b + o):512 * (b + o) + n], T.cw[:, 128 * o:128 * o + 128], T.sw[:, 128 * o:128 * o + 128],
-                 T.c2[:, j:j + n], T.s2[:, j:j + n], after=toks) for o in range(O)]
+        ty = {o: mm(T.ps[:, 512 * (b + o):512 * (b + o) + n], T.cw[:, 128 * o:128 * o + 128], T.sw[:, 128 * o:128 * o + 128],
+                    T.c2[:, j:j + n], T.s2[:, j:j + n], after=toks) for o in (0, 2, 1, 3)}
         return [(T.yy[:, 512 * o + j:512 * o + j + n], T.ps[:, 512 * (b + o):512 * (b + o) + n], ty[o]) for o in range(O)]
 
     def result(out, ps, tok):
         return act(out, ps, F.Copy, after=[tok])
 
-    sme = replicated(f2, T.pme, vpn)
-    who(f2, T.pme, spn)
-    here = [result(*r) for r in products(H * f2, H, 4, vw, *p2)]
+    ty = products(H * f2, H, 4, vw, *p2)
+    here = {o: result(*ty[o]) for o in (0, 2, 1, 3)}
 
-    v = vec("tt", T.t1[:], msg[:], T["m%d" % other][:], A.add, after=[*smsg, arrm[other]])
-    e = [vec("ts", T.pou[:, i:i + 1], T.t1[:, i:i + 1], T["m%d" % mate][:, i:i + 1], T["m%d" % (other ^ 1)][:, i:i + 1],
-             A.add, A.add, after=[v, arrm[mate], arrm[other ^ 1]]) for i in range(4)]
+    for h, op in ((f2, A.min), (k2, A.add)):
+        v = vec("tt", T.t1[:, 2 * h:2 * h + 2], T.mb[:, 508 + 2 * h:510 + 2 * h], T["m%d" % mate][:, 2 * h:2 * h + 2], op,
+                after=[*smsg, arrm[mate]])
+    sme = replicated(f2, T.pme, vpn)
+    for i in range(4):
+        e = vec("ts", T.pou[:, i:i + 1], T["m%d" % other][:, i:i + 1], T["m%d" % (other ^ 1)][:, i:i + 1], T.t1[:, i:i + 1],
+                A.add if i // 2 == f2 else A.min, A.add, after=[v, arrm[other], arrm[other ^ 1]])
     ty = products(H * k2, H, 0, arr2)
 
     def half(i):
-        return vec("copy", T.yy[:, 512 + H * k2 + 128 * i:640 + H * k2 + 128 * i], T.ps[:, 512 + 128 * i:640 + 128 * i],
-                   after=[ty[1][2]])
+        return vec("copy", T.yy[:, 1024 + H * k2 + 128 * i:1152 + H * k2 + 128 * i], T.ps[:, 1024 + 128 * i:1152 + 128 * i],
+                   after=[ty[2][2]])
 
-    s = replicated(k2, T.pth, arrp)
-    v2 = to_list(e[1::2], T.val2, T.q2, 32, 800, 2,
-                 (lambda: turned(f2, sme), lambda tok: who(k2, T.pth, arrp), lambda: turned(k2, s), lambda: half(0)))[1]
-    there = [half(1) if o == 1 else result(*r) for o, r in enumerate(ty)]
+    def theirs(tok):
+        replicated(k2, T.pth, arrp)
+        got.append(who(k2, T.pth[0:64, 8:9]))
+
+    got = []
+    v2 = to_list([e], T.val2, T.q2, 32, 800, 1, (lambda: turned(f2, sme), theirs, lambda: turned(k2, got[0]), lambda: half(0)))[1]
+    there = {o: result(*ty[o]) for o in (0, 1, 3)}
+    vec("ts", T.q2[:, 16:32], T.zs[:].indirect(T.fo[:, 2:3]), 256.0, None, A.add)
+    there[2] = half(1)
 
     def store(y, out, in_, *toks):
         wait(y, *toks)
         inc("dy%d" % (y == "s"), q[y].dma_start(out, in_), 16)
 
-    def winners(o, j0, j1, on_vector):
+    def winners(o, j0=0, j1=16):
         ab = T.ysb[:, K * o + 16 * j0:K * o + 16 * j1], T.yy[:, 512 * o:512 * o + 512].indirect(T.q2[:, j0:j1])
         toks = [v2, here[o], there[o]]
-        return vec("copy", *ab, after=toks) if on_vector else act(*ab, F.Copy, after=toks)
+        return vec("copy", *ab, after=toks) if o % 2 == 0 else act(*ab, F.Copy, after=toks)
 
-    done = [winners(o, 0, 16, o < 2) for o in range(O)]
+    parts = [("y", 0, 128, winners(0, 0, 8)), ("y", 128, 256, winners(0, 8, 16)), ("y", 256, 512, winners(1)),
+             ("s", 512, 1024, winners(2), winners(3))]
     v = vec("ts", T.idf[:], T.tab[:].indirect(T.q2[:, 16:20]), T.up256[:], None, A.add)
-    for o in (0, 2, 1, 3):
-        store("yyys"[o], T.y[:, K * o:K * o + K], T.ysb[:, K * o:K * o + K], done[o])
+    for y, j0, j1, *toks in parts:
+        store(y, T.y[:, j0:j1], T.ysb[:, j0:j1], *toks)
     store("y", T.id[:], T.idf[0:128:16, :], v)
 
     wait("g", out0, out1, outn, outk, out2, outm, outp, arr0, arr1, arr2, arrn, arrp, *arrk.values(), *arrm.values(),

from concourse.bass import DstId, RemoteDMATransfer
from concourse.mybir import dt, AluOpType, ActivationFunctionType

K, O = 256, 4
H = 256
SCRATCH = {"ps": ("psum", [128, 4096], "float32")}


def _bufs(dtype, **widths):
    for name, n in widths.items():
        SCRATCH[name] = ("sbuf", [128, n], dtype)


_bufs("float8_e4m3fn_x4", cx=512, cq=128, cu=128, cw=512, c1=512, c2=512)
_bufs("uint8", sx=512, sq=128, su=128, sw=512, s1=512, s2=512)
_bufs("bfloat16", xb=2048, wb=2048, up=512, neg=128, dm=128, fl=2048, cs=256, ce=512, f1=256, g1=128,
      val=64, val2=64, win=800, wt=544, zs=136, rz=136, iot=256, rep=512, tab=512,
      nme=8, nin=8, nab=8, nth=8, pme=16, pth=16)
_bufs("float32", sc4=4, nd=4, th=512, pl=4, vb=64, vb2=64, hc=1, fx=1, fy=1, fz=1, fw=1, k16=16, k256=16, kb=2,
      k32=8, rv=256, rows=512, sg=32, sgt=32, h1=16, h2=16, dn=8, h3=8, h4=8, k0=2, k1=2, k2=2, k3=2, m0=4, m1=4, m2=4,
      m3=4, mb=512, cp=2, t1=4, idf=64, yy=2048, ysb=1024, fu=1, fv=1, up256=1)
_bufs("int32", ip=16, i15=16, c16=16, y17=1, a14=1, a112=1, a48=1, a2=1)
_bufs("uint16", u0=8, pou=4, fo=4, lst=32, q1=16, q2=32)
SEMAPHORES = ["cv", "ca", "ct", "cp", "du", "dx0", "dx1", "dx2", "dx3", "dw", "dy0", "dy1", "a0", "o0", "a1", "o1", "a2", "o2",
              "on", "ok", "om", "op", "an", "ap", "ak0", "ak1", "ak2", "ak3", "am0", "am1", "am2", "am3"]
STEP, TINY = 1.125 * 2.0 ** -24, 2.0 ** -124


def rank_program(g, core, T, topo):
    rank = T.rank_of(core)
    if rank is None:
        return
    A, F = AluOpType, ActivationFunctionType
    q = {"v": g.vector, "s": g.scalar, "t": g.tensor, "g": g, "y": g.sync}
    cnt, seen = {}, {}

    def inc(sem, ins, n=1):
        ins.then_inc(T.sem[sem], n)
        cnt[sem] = cnt.get(sem, 0) + n
        return (sem, cnt[sem])

    def wait(qn, *toks):
        best = {}
        for t in toks:
            best[t[0]] = max(best.get(t[0], 0), t[1])
        for sem, v in best.items():
            if seen.get((qn, sem), 0) < v:
                q[qn].wait_ge(T.sem[sem], v)
                seen[(qn, sem)] = v

    def vec(name, *args, after=()):
        wait("v", *after)
        calls = {"copy": g.vector.tensor_copy, "tt": g.vector.tensor_tensor, "ts": g.vector.tensor_scalar,
                 "set": g.vector.memset, "scan": g.vector.tensor_tensor_scan, "tr": g.vector.transpose,
                 "quant": g.vector.quantize_mx}
        return inc("cv", calls[name](*args))

    def act(out, in_, func, after=(), **kw):
        wait("s", *after)
        return inc("ca", g.scalar.activation(out, in_, func, **kw))

    def mm(out, a, sa, b, sb, after=()):
        wait("t", *after)
        return inc("ct", g.tensor.matmul_mx(out, a, sa, b, sb, True, True))

    mate, other = rank ^ 1, rank ^ 2
    lower = rank < mate
    a0 = 0 if lower else H
    b0 = H - a0
    f2 = 0 if rank < other else 1
    k2 = 1 - f2

    du = inc("du", g.scalar.dma_start(T.up[:, 0:8], T.u[:, 0:8]), 16)
    dx = [inc("dx%d" % t, g.sync.dma_start(T.xb[:, 512 * t:512 * t + 512], T.x[:, 512 * t:512 * t + 512]), 16)
          for t in range(4)]
    dw = inc("dw", g.sync.dma_start(T.wb[:], T.w[:]), 16)

    vneg = vec("set", T.neg[:], -1.0)
    f = {"allow_small_or_imprecise_dtypes": True}
    pip = inc("cp", g.iota(T.ip[:], [[0, 16]], 0, 1))
    pvb = inc("cp", g.iota(T.vb[:], [[128, 4], [1, 16]], 0, 0, **f))
    wait("g", vneg)
    pdm = inc("cp", g.affine_select(T.dm[:], T.neg[:], [[-1, 128]], A.is_gt if lower else A.is_ge, 0.0, 0, 1))
    pc16 = inc("cp", g.iota(T.c16[:], [[16, 16]], 0, 0))
    sg = -1 if lower else 1
    wait("g", pc16)
    for r in range(4):
        run = slice(32 * r, 32 * r + 32)
        inc("cp", g.iota(T.kb[run, :], [[32 * sg, 2]], 64 * r * sg + (255 if lower else 0), sg, **f))
        inc("cp", g.iota(T.k32[run, :], [[32, 8]], -256, 1, **f))
        pvb2 = inc("cp", g.iota(T.vb2[run, :], [[256, 2], [32, 2], [1, 16]], 32 * r - 256, 0, **f))
    wait("g", pvb2)
    inc("cp", g.iota(T.iot[0:64, :], [[1, 256]], -256, 0, **f))
    inc("cp", g.iota(T.up256[0:64, :], [[0, 1]], 0, 0, **f))
    piot = inc("cp", g.iota(T.up256[64:128, :], [[0, 1]], 256, 0, **f))
    w0 = 32 if lower else 32 + H
    vec("set", T.up[:, 8:512], 0.0)
    vec("set", T.u0[:], 0)
    vec("set", T.pme[0:64, :], 0.0)
    v1 = vec("set", T.rz[:], 1.0)
    vwin = vec("set", T.win[:, w0 - 16:w0 + 272], 0.0)
    vec("ts", T.i15[:], T.ip[:], 15, None, A.bitwise_and, after=[pip])
    for out, bits in ((T.y17, 17), (T.a14, 14), (T.a112, 112), (T.a48, 48), (T.a2, 2)):
        va = vec("ts", out[:], T.ip[:, 0:1], bits, None, A.bitwise_and)
    vrz = vec("set", T.rz[:, 0:136:8], 0.0, after=[v1])
    vec("tt", T.hc[:], T.ip[:, 0:1], T.i15[:, 0:1], A.subtract, after=[va])
    v = vec("ts", T.fx[:], T.y17[:], 1, 72.0, A.is_equal, A.mult)
    vec("ts", T.fy[:], T.y17[:], 16, 64.0, A.is_equal, A.mult)
    vec("ts", T.fz[:], T.a14[:], 4.0, 7.0, A.mult, A.add)
    vec("ts", T.fw[:], T.a112[:], 0.5, 7.0, A.mult, A.add)
    vec("ts", T.fu[:], T.a2[:], 4.0, 7.0, A.mult, A.add)
    vec("tt", T.fv[:], T.a48[:], T.fx[:], A.add, after=[v])
    vf = vec("tt", T.k16[:], T.i15[:], T.c16[:], A.add, after=[pc16])
    vu = vec("quant", T.cq[:], T.sq[:], T.up[:], after=[du, v1])

    def quantised(t):
        return vec("quant", T.cx[:, 128 * t:128 * t + 128], T.sx[:, 128 * t:128 * t + 128], T.xb[:, 512 * t:512 * t + 512],
                   after=[dx[t]])

    def down(t, *toks):
        b = 512 * (2 + t % 2)
        return mm(T.ps[:, b:b + 128], T.cx[:, 128 * t:128 * t + 128], T.sx[:, 128 * t:128 * t + 128], T.cq[:], T.sq[:], after=toks)

    def along(p, j0, j1, *toks):
        return mm(T.ps[:, p:p + j1 - j0], T.cu[:], T.su[:], T.cx[:, j0:j1], T.sx[:, j0:j1], after=toks)

    ROW_V, ROW_S = (0, 128, 512, 2048), (None, 2560, 3072, 3584)

    def column(t, tx):
        ps = T.ps[:, 512 * (2 + t % 2):512 * (2 + t % 2) + 1]
        return (act(T.sc4[:, t:t + 1], ps, F.Copy, after=[tx]), act(T.nd[:, t:t + 1], ps, F.Abs, scale=STEP, bias=TINY))

    def inside(t, sc):
        return act(T.th[:, 128 * t:128 * t + 128], T.dm[:], F.Identity, after=[*sc, pdm], scale=T.nd[:, t:t + 1],
                   bias=T.sc4[:, t:t + 1])

    def signs(t, b, *toks):
        return act(T.fl[:, 512 * t + 128 * b:512 * t + 128 * b + 128], T.ps[:, ROW_S[b]:ROW_S[b] + 128], F.Sign, scale=-1.0,
                   bias=T.sc4[:, t:t + 1], after=toks)

    def counted(t, j0, j1, i, tok):
        fl = T.fl[:, 512 * t + j0:512 * t + j1]
        how = (F.Relu, -1.0, 0.0) if lower else (F.Sign, 1.0, 1.0)
        return act(fl, fl, how[0], scale=how[1], bias=how[2], accum_out=T.pl[:, i:i + 1], after=[tok])

    def plain(t, j0, j1, *toks):
        p = ROW_V[j0 // 128]
        if j1 <= 128 * t:
            op = A.is_ge if lower else A.is_lt
        else:
            op = A.is_gt if lower else A.is_le
        return vec("ts", T.fl[:, 512 * t + j0:512 * t + j1], T.ps[:, p:p + j1 - j0], T.sc4[:, t:t + 1], None, op, after=toks)

    def diag(t, *toks):
        return vec("tt", T.fl[:, 640 * t:640 * t + 128], T.ps[:, ROW_V[t]:ROW_V[t] + 128], T.th[:, 128 * t:128 * t + 128],
                   A.is_gt if lower else A.is_le, after=toks)

    def halves(z, j, tok, n, start=0.0):
        return vec("scan", T.cs[:, j:j + n], T.fl[:, z:z + n], T.fl[:, z + n:z + 2 * n], start, A.add, A.add, after=[tok])

    def row_sum(t, tok):
        z, j = 512 * t, 256 * (t % 2)
        return vec("scan", T.ce[:, j:j + 256], T.fl[:, z:z + 256], T.fl[:, z + 256:z + 512], -256.0, A.add, A.add, after=[tok])

    def to_list(toks, val, out, w0, w1, fo, beside):
        e = vec("copy", T.win[:, 32:w1].indirect(T.pou[:]), val[:], after=[*toks, vval, vwin])
        beside[0]()
        v = vec("tr", T.wt[:, 0:256], T.win[:, w0:w0 + 256], after=[e])
        e = vec("tr", T.wt[:, 256:544], T.win[:, w0 - 16:w0 + 272])
        got = beside[1](v)
        runs = [(0, 64, 2, 1), (2, 64, 0, 1), *[(d, 32, d ^ 1, 2) for d in range(4)], *[(d, 32, d ^ 3, 3) for d in range(4)]]
        toks = []
        for i, (d, m, src, j) in enumerate(runs):
            ab = T.wt[32 * d:32 * d + m, 4 * j:544:16], T.wt[32 * src:32 * src + m, 0:544:16]
            toks.append(vec("copy", *ab, after=[e]) if i < 6 else act(*ab, F.Copy, after=[e]))
        beside[2]()
        e = vec("scan", T.zs[:], T.rz[:], T.wt[:, 0:544:4], 0.0, A.mult, A.add, after=[*toks, vrz])
        beside[3]()
        return got, vec("ts", out[:, 0:16 * fo], T.zs[:].indirect(T.fo[:, 0:fo]), 256.0, None, A.add, after=[e, vfo])

    def pick(c_to, s_to, j, c, s, off, *toks, n=K):
        v = vec("copy", c_to[:, j:j + n].bitcast(dt.uint32), c[:].bitcast(dt.uint32).indirect(off), after=toks)
        return v, act(s_to[:, j:j + n], s[:].indirect(off), F.Copy, after=toks)

    def offsets(*which):
        for i in which:
            x, w = ((T.fx, T.fz), (T.fx, T.fw), (T.fv, T.fu))[i]
            v = vec("ts", T.fo[:, i:i + 1], x[:], T.fy[:], w[:], A.add, A.add, after=[vf])
        return v

    t0 = down(0, vu, quantised(0))
    vqu = pick(T.cu, T.su, 0, T.cq, T.sq, T.u0[:], vu, n=128)
    t1 = down(1, quantised(1))
    r01 = along(ROW_V[0], 0, 256, *vqu)
    sc0 = column(0, t0)
    th0 = inside(0, sc0)
    sc1 = column(1, t1)
    t2 = down(2, quantised(2), sc0[1])
    x1 = along(ROW_S[1], 128, 256)
    r2, x2 = along(ROW_V[2], 256, 384), along(ROW_S[2], 256, 384)
    vfo = offsets(0, 1)
    vval = vec("ts", T.val[:], T.vb[:], T.hc[:], -256.0, A.add, A.add, after=[pvb])
    t3 = down(3, quantised(3), sc1[1])
    r3, x3 = along(ROW_V[3], 384, 512), along(ROW_S[3], 384, 512)
    sc2 = column(2, t2)
    tall = along(1024, 0, 512, sc2[1])
    th1 = inside(1, sc1)
    signs(0, 1, x1)
    th2 = inside(2, sc2)
    sc3 = column(3, t3)
    signs(0, 2, x2)
    s0 = signs(0, 3, x3)
    th3 = inside(3, sc3)
    s1 = signs(1, 3)
    s0, s1 = counted(0, 128, 512, 0, s0), counted(1, 384, 512, 1, s1)
    srows = act(T.rows[:], T.ps[:, 1024:1536], F.Copy, after=[tall])
    d0 = diag(0, th0, r01)
    plain(1, 0, 128, sc1[0])
    halves(0, 0, d0, 64)
    plain(2, 0, H, sc2[0])
    diag(1, th1)
    d1 = plain(1, H, 384, r2)
    plain(2, 384, 512, r3)
    d2 = diag(2, th2)
    plain(3, 0, H, sc3[0])
    plain(3, H, 384)
    d3 = diag(3, th3)
    v = halves(512, 64, d1, 192, -128.0)
    row_sum(2, d2)
    e = row_sum(3, d3)
    vec("ts", T.pou[:, 0:1], T.cs[:, 63:64], T.pl[:, 0:1], None, A.add, after=[s0, v])
    v = vec("ts", T.pou[:, 1:2], T.cs[:, 255:256], T.pl[:, 1:2], 128.0, A.add, A.add, after=[s1])
    vpl = vec("ts", T.pou[:, 2:4], T.ce[:, 255:512:256], 256.0, None, A.add, after=[e])

    def nothing(*toks):
        return None

    def numbers(tok):
        return vec("tt", T.nme[:], T.wt[:, 0:256:32], T.wt[:, 16:256:32], A.add, after=[tok])

    vnum, ql = to_list((v, vpl), T.val, T.lst, w0, 544, 2, (nothing, numbers, nothing, nothing))

    def note(dst, src, to, what, *toks):
        rid, pid, _ = topo.addr(T.cores[to])
        wait("g", *toks)
        g.remote_dma(dst, src, T.sem["a" + what], T.sem["o" + what], pid, rid, topo.mask(core, T.cores[to]))
        n = len(topo.engines(core, T.cores[to]))
        return ("a" + what, n), ("o" + what, n)

    def tell(what, me, to, *toks):
        m, n = topo.mask(core, T.cores[other]), len(topo.engines(core, T.cores[other]))
        ids = [DstId(rid=topo.addr(T.cores[r])[0], pnc=topo.addr(T.cores[r])[1]) for r in to]
        tr = RemoteDMATransfer(dst_ids=ids, dma_engine_mask=m, remote_sem=T.sem["a%s%d" % (what, rank)], src=me,
                               dsts=[T["%s%d" % (what, rank)][:]] * len(to))
        wait("g", *toks)
        g.remote_dma_fused([tr], local_sem=T.sem["o" + what])
        return {r: ("a%s%d" % (what, r), n) for r in to}, ("o" + what, n)

    arrn, outn = note(T.nin[:], T.nme[:], mate, "n", vnum)
    s = act(T.sg[:], T.rows[:].indirect(T.lst[:, 16:18]), F.Copy, after=[ql, srows])
    p0 = pick(T.c1, T.s1, a0, T.cx, T.sx, T.lst[:, 0:8], ql, n=128)
    vk = vec("tr", T.sgt[:], T.sg[:], after=[s])
    kme = T.sgt[:, 15:17]

    cc = [T.c1[:, a0 + 128 * i:a0 + 128 * i + 128].bitcast(dt.uint8) for i in (0, 1)]
    note(cc[0], cc[0], mate, "0", p0[0])
    arrk, outk = tell("k", kme, (other, other ^ 1, mate), vk)
    p1 = pick(T.c1, T.s1, a0 + 128, T.cx, T.sx, T.lst[:, 8:16], ql, n=128)
    arr0, out0 = [(s, 2 * n) for s, n in note(T.s1[:, a0:a0 + K], T.s1[:, a0:a0 + K], mate, "0", p1[1])]
    arr1, out1 = note(cc[1], cc[1], mate, "1", p1[0])
    prep = inc("cp", g.iota(T.rep[64:128, :], [[0, 512]], 0, 0, **f))

    t = mm(T.ps[:, 0:256], T.cu[:], T.su[:], T.c1[:, a0:a0 + H], T.s1[:, a0:a0 + H], after=p1)
    srv = act(T.rv[:], T.ps[:, 0:256], F.Copy, after=[t])
    vec("ts", T.val2[:], T.vb2[:], T.hc[:], None, A.add, after=[pvb2])
    vec("ts", T.k256[:], T.k16[:], -256.0, None, A.add)
    offsets(2)
    vw = vec("quant", T.cw[:], T.sw[:], T.wb[:], after=[dw])
    v = vec("tt", T.nab[64:128, :], T.nin[64:128, :], T.nin[0:64, :], A.add, after=[arrn])
    vwin = vec("set", T.win[:, 16:304], 0.0)
    for d in (64, 96):
        vec("tt", T.nth[d:d + 32, :], T.nab[64:96, :], T.nab[96:128, :], A.add, after=[v])
    nl, nu = T.zs[64:128, 7:64:8], T.nth[64:128, :]
    nl, nu = (nl, nu) if lower else (nu, nl)

    def kk(r):
        return T["k%d" % r]

    def who(h, m, *toks):
        return vec("ts", T.tab[0:64, H * h:H * h + H], T.iot[0:64, :], m, 2.0 * h, A.is_ge, A.add, after=[piot, *toks])

    msg = T.mb[:, 508:512]
    vcp = vec("tt", T.cp[:], kk(other)[:], kk(other ^ 1)[:], A.max, after=[arrk[other], arrk[other ^ 1]])
    s = [act(T.fl[:, H * i:H * i + H], T.rv[:], F.Sign, scale=-1.0, bias=T.cp[:, i:i + 1], after=[vcp, srv]) for i in (0, 1)]
    how = (F.Sign, 1.0) if f2 == 0 else (F.Relu, 0.0)
    smsg = [act(T.fl[:, 512 + H * i:768 + H * i], T.fl[:, H * i:H * i + H], how[0], scale=-1.0, bias=how[1],
                accum_out=T.mb[:, 508 + 2 * k2 + i:509 + 2 * k2 + i], after=[s[i]]) for i in (0, 1)]
    c = [vec("ts", T.fl[:, 1024 + H * i:1280 + H * i], T.rv[:], kk(mate)[:, i:i + 1], None, A.is_ge if lower else A.is_gt,
             after=[arrk[mate], srv]) for i in (0, 1)]

    for i, arr in enumerate((arr0, arr1)):
        j, theirs = b0 + 128 * i, T.ps[:, 512 * (1 + i):512 * (1 + i) + 128]
        row = mm(theirs, T.cu[:], T.su[:], T.c1[:, j:j + 128], T.s1[:, j:j + 128], after=[arr, srows])
        rows = T.rv[:, 128 * i:128 * i + 128], theirs
        v = vec("tt", T.f1[:, 128 * i:128 * i + 128], *(rows if lower else rows[::-1]), A.is_ge, after=[row])

    def place(i):
        z = 1024 + H * i
        return vec("scan", T.mb[:, 2 * f2 + i:512:4], T.fl[:, z:z + 128], T.fl[:, z + 128:z + 256], T.kb[:, i:i + 1],
                   A.add, A.add, after=[c[i]])

    place(0)
    mine = T.g1[:, 127:128]
    vm1 = vec("scan", T.g1[:], T.f1[:, 0:128], T.f1[:, 128:256], -256.0, A.add, A.add, after=[v])
    arrm, outm = tell("m", msg, (mate, other, other ^ 1), place(1), *smsg)
    v = vec("ts", T.h1[:], T.k256[:], mine, 256.0, A.is_ge, A.mult, after=[vm1])
    vec("tt", T.dn[64:128, :], nu, nl, A.subtract)
    vh = vec("ts", T.h3[64:128, :], T.k32[64:128, :], T.g1[64:128, 127:128], None, A.is_ge)
    v = vec("tt", T.h2[:], T.k16[:], T.h1[:], A.add, after=[v])
    who(f2, T.g1[0:64, 127:128])
    vh = vec("tt", T.h4[64:128, :], T.h3[64:128, :], T.dn[64:128, :], A.mult, after=[vh])
    vc = vec("copy", T.q1[:], T.h2[:], after=[v])
    vec("copy", T.pme[:, 8:9], mine)
    vpn = vec("tt", T.pme[64:128, 0:8], T.h4[64:128, :], nl, A.add, after=[vh])
    j = H * f2
    p2 = pick(T.c2, T.s2, j, T.c1, T.s1, T.q1[:], vc, arr0, arr1, *p1)

    arrp, outp = note(T.pth[:, 0:9], T.pme[:, 0:9], other, "p", vpn)
    cc = T.c2[:, j:j + K].bitcast(dt.uint8)
    note(cc, cc, other, "2", p2[0])
    arr2, out2 = [(s, 2 * n) for s, n in note(T.s2[:, j:j + K], T.s2[:, j:j + K], other, "2", p2[1])]

    def replicated(h, src, *toks):
        for j in (0, 16):
            s = vec("copy", T.rep[64:128, H * h + j:H * h + H:32], src[64:128, 0:8], after=[prep, *toks])
        return s

    def turned(h, tok):
        return vec("tr", T.tab[64:128, H * h:H * h + H], T.rep[64:128, H * h:H * h + H], after=[tok])

    def products(j, n, b, *toks):
        ty = {o: mm(T.ps[:, 512 * (b + o):512 * (b + o) + n], T.cw[:, 128 * o:128 * o + 128], T.sw[:, 128 * o:128 * o + 128],
                    T.c2[:, j:j + n], T.s2[:, j:j + n], after=toks) for o in (0, 2, 1, 3)}
        return [(T.yy[:, 512 * o + j:512 * o + j + n], T.ps[:, 512 * (b + o):512 * (b + o) + n], ty[o]) for o in range(O)]

    def result(out, ps, tok):
        return act(out, ps, F.Copy, after=[tok])

    ty = products(H * f2, H, 4, vw, *p2)
    here = {o: result(*ty[o]) for o in (0, 2, 1, 3)}

    for h, op in ((f2, A.min), (k2, A.add)):
        v = vec("tt", T.t1[:, 2 * h:2 * h + 2], T.mb[:, 508 + 2 * h:510 + 2 * h], T["m%d" % mate][:, 2 * h:2 * h + 2], op,
                after=[*smsg, arrm[mate]])
    sme = replicated(f2, T.pme, vpn)
    for i in range(4):
        e = vec("ts", T.pou[:, i:i + 1], T["m%d" % other][:, i:i + 1], T["m%d" % (other ^ 1)][:, i:i + 1], T.t1[:, i:i + 1],
                A.add if i // 2 == f2 else A.min, A.add, after=[v, arrm[other], arrm[other ^ 1]])
    ty = products(H * k2, H, 0, arr2)

    def half(i):
        return vec("copy", T.yy[:, 1024 + H * k2 + 128 * i:1152 + H * k2 + 128 * i], T.ps[:, 1024 + 128 * i:1152 + 128 * i],
                   after=[ty[2][2]])

    def theirs(tok):
        replicated(k2, T.pth, arrp)
        got.append(who(k2, T.pth[0:64, 8:9]))

    got = []
    v2 = to_list([e], T.val2, T.q2, 32, 800, 1, (lambda: turned(f2, sme), theirs, lambda: turned(k2, got[0]), lambda: half(0)))[1]
    there = {o: result(*ty[o]) for o in (0, 1, 3)}
    vec("ts", T.q2[:, 16:32], T.zs[:].indirect(T.fo[:, 2:3]), 256.0, None, A.add)
    there[2] = half(1)

    def store(y, out, in_, *toks):
        wait(y, *toks)
        inc("dy%d" % (y == "s"), q[y].dma_start(out, in_), 16)

    def winners(o, j0=0, j1=16):
        ab = T.ysb[:, K * o + 16 * j0:K * o + 16 * j1], T.yy[:, 512 * o:512 * o + 512].indirect(T.q2[:, j0:j1])
        toks = [v2, here[o], there[o]]
        return vec("copy", *ab, after=toks) if o % 2 == 0 else act(*ab, F.Copy, after=toks)

    parts = [("y", 0, 128, winners(0, 0, 8)), ("y", 128, 256, winners(0, 8, 16)), ("y", 256, 512, winners(1)),
             ("s", 512, 1024, winners(2), winners(3))]
    v = vec("ts", T.idf[:], T.tab[:].indirect(T.q2[:, 16:20]), T.up256[:], None, A.add)
    for y, j0, j1, *toks in parts:
        store(y, T.y[:, j0:j1], T.ysb[:, j0:j1], *toks)
    store("y", T.id[:], T.idf[0:128:16, :], v)

    wait("g", out0, out1, outn, outk, out2, outm, outp, arr0, arr1, arr2, arrn, arrp, *arrk.values(), *arrm.values(),
         *[(s, n) for s, n in cnt.items()])
